import numpy as np, ml_dtypes
CORES = [6,15,38,47]
N = 4
import mx_ref
BF = ml_dtypes.bfloat16
def gentries(a):
    return np.ascontiguousarray(a.reshape(8, 16, -1).transpose(0, 2, 1)).reshape(8, -1)
def gtable(e):
    e = np.asarray(e); return np.ascontiguousarray(e.reshape(8, -1, 16).transpose(0, 2, 1)).reshape(128, -1).astype(np.int32)
def gcols(t, e):
    v = np.concatenate([t.reshape(8, 16, -1, 4), np.zeros((8, 16, 1, 4), BF)], axis=2)
    return np.ascontiguousarray(np.stack([v[g][:, e[g]] for g in range(8)])).reshape(128, -1)
def tile(rs):
    return np.stack(rs, axis=2).reshape(128, -1).astype(BF)
def cut(t, i, w=512):
    return t[:, w * i:w * i + w]
def pick(q, e):
    c = np.concatenate([q[0].reshape(128, -1, 4), np.zeros((128, 1, 4), np.uint8)], axis=1); s = np.concatenate([q[1], np.ones((16, 1), np.uint8)], axis=1)
    return (np.ascontiguousarray(c[:, e].reshape(128, -1)), np.ascontiguousarray(s[:, e]))
def join(*qs):
    return (np.concatenate([q[0] for q in qs], axis=1), np.concatenate([q[1] for q in qs], axis=1))
def put(q, e, v):
    c, s = q[0].reshape(128, -1, 4).copy(), q[1].copy(); c[:, e] = v[0].reshape(128, -1, 4); s[:, e] = v[1]
    return (c.reshape(128, -1), s)
def pk(c, s):
    return (np.ascontiguousarray(c), mx_ref.live(s))
def emit(q):
    return q[0], q[1]
def packed(v, rng):
    q = [mx_ref.quantize(np.ascontiguousarray(v[r])) for r in range(N)]
    return np.stack([a for a, b in q]), np.stack([mx_ref.plane(b, rng) for a, b in q])
def values_of_codes():
    e, c = np.zeros((128, 128, 4), np.float32), np.zeros((128, 2, 4), np.uint8)
    e[np.arange(128), np.arange(128), 0] = 1
    c[:127, :, 0] = np.arange(256).reshape(2, 128).T[:127]
    return mx_ref.matmul(mx_ref.quantize(e.reshape(128, 512).astype(BF)), (c.reshape(128, 8), np.full((16, 2), 127, np.uint8))).T.reshape(-1).astype(np.float64)
CODE_VALUE, SCALE_VALUE = values_of_codes(), 2.0 ** (np.arange(256) - 127.0)
def decode(q):
    return (CODE_VALUE[q[0]].reshape(16, 8, -1, 4) * SCALE_VALUE[q[1]][:, None, :, None] + 0.0).reshape(128, -1).astype(np.float32)
def f(rng, *shape):
    return mx_ref.flush((rng.standard_normal(shape, dtype=np.float32) * np.exp2(rng.integers(-2, 3, shape[:-1] + (1,)))).astype(BF))
def wide(rng, *shape, cols=0):
    v = rng.standard_normal(shape, dtype=np.float32) * np.exp2(rng.integers(-12, 13, shape)).astype(np.float32)
    if cols: v *= np.repeat(np.exp2(rng.integers(-cols, cols + 1, shape[:-2] + (1, shape[-1] // 4))) * (rng.random(shape[:-2] + (1, shape[-1] // 4)) > 0.0625), 4, axis=-1).astype(np.float32)
    return mx_ref.flush(v.astype(BF))
T, P, H = 384, 480, 3
def trim(v):
    v = v.astype(np.float32)
    v[np.abs(v) < np.float32(2.0 ** -16)] = 0
    return v.astype(BF)
def numbers_of(rng):
    return {"x": trim(f(rng, N, 128, 4 * T)), "k": trim(f(rng, N, 128, 4 * P)), "u": np.array(f(rng, N, 128, 512)), "v": np.array(f(rng, N, 128, 512))}
def weights(rng, w):
    c, p = packed(np.stack([w] * N), rng)
    return {"wc": c, "ws": p}
def still(rng):
    w = np.zeros((128, 4, 128, 4), np.float32)
    i = np.arange(128)
    for b in range(4): w[i, b, i, b] = 32
    return weights(rng, w.reshape(128, 2048).astype(BF))
def chase(nx, e):
    return {"nx": np.ascontiguousarray(nx).astype(np.int32), "st": np.stack([gtable(e[r]) for r in range(N)])}
def setup_inputs(rng):
    return {**numbers_of(rng), **weights(rng, np.array(f(rng, 128, 2048))), **chase(rng.integers(0, P, (N, 8, 2 * P)), rng.integers(0, P, (N, 8, T)))}
def setup_inputs_ties(rng):
    d = numbers_of(rng)
    x, k, u = d["x"].reshape(N, 128, T, 4), d["k"].reshape(N, 128, P, 4), d["u"].reshape(N, 128, 128, 4)
    k[:, :, ::2] = 0
    c = np.stack([rng.permutation(T) % 4 for r in range(N)])
    e = rng.integers(0, P, (N, 8, T))
    e = np.where(c[:, None, :] == 1, e // 2 * 2, e)
    for r in range(N):
        for g in rng.permutation(8)[:2]: u[r, :, 16 * g] = 0
        o = gcols(k[r].reshape(128, 4 * P), e[r]).reshape(128, T, 4)
        o = (np.float32(0.0) - o.astype(np.float32)).astype(BF)
        x[r][:, c[r] == 1] = 0
        x[r][:, c[r] == 2] = o[:, c[r] == 2]
    a = rng.integers(0, P, (N, 8, P))
    a = np.where(np.arange(P) % 2 == 0, a // 2 * 2, a)
    b = (a + 2 * rng.integers(1, P // 2, (N, 8, P))) % P
    return {"x": x.reshape(N, 128, 4 * T), "k": k.reshape(N, 128, 4 * P), "u": u.reshape(N, 128, 512), "v": d["v"], **weights(rng, np.array(f(rng, 128, 2048))), **chase(np.stack([a, b], axis=3).reshape(N, 8, 2 * P), e)}
def setup_inputs_sizes(rng):
    def columns(c):
        tiny = c % 2 == 0
        s = np.where(tiny, 2.0 ** -29, 2.0 ** 30) * np.where(c >= 2, -1.0, 1.0)
        a = 0.55 + 0.4 * rng.random((N, 128, c.shape[1], 4))
        a[:, ::16, :, 0] = np.where(tiny[:, None, :], 0.5625, a[:, ::16, :, 0])
        a[:, 8::16, :, 0] = np.where(tiny[:, None, :], 0.625, a[:, 8::16, :, 0])
        return (a * s[:, None, :, None]).astype(np.float32).astype(BF).reshape(N, 128, 4 * c.shape[1])
    d = numbers_of(rng)
    c = np.stack([rng.permutation(T) % 4 for r in range(N)])
    i = np.arange(P) % 4
    u = d["u"].reshape(N, 128, 128, 4)
    u[:, :, ::16] = 0
    for r in range(N):
        o = rng.permutation(8)
        for g in range(8):
            s = 1.0 if o[g] % 2 == 0 else -1.0
            if o[g] < 4:
                u[r, 16 * g, 16 * g, 0] = s * 1.125 * 2.0 ** -30
                u[r, 16 * g + 8, 16 * g, 0] = -s * 2.0 ** -30
            else: u[r, :, 16 * g] = (s * 2.0 ** 30 * (0.55 + 0.4 * rng.random((128, 4)))).astype(np.float32).astype(BF)
    a = 4 * rng.integers(0, P // 4, (N, 8, P)) + i
    b = (a + 4 * rng.integers(1, P // 4, (N, 8, P))) % P
    e = 4 * rng.integers(0, P // 4, (N, 8, T)) + c[:, None, :]
    return {"x": columns(c), "k": columns(np.stack([i] * N)), "u": u.reshape(N, 128, 512), "v": d["v"], **still(rng), **chase(np.stack([a, b], axis=3).reshape(N, 8, 2 * P), e)}
def setup_inputs_crowd(rng):
    d = setup_inputs(rng)
    o = rng.permutation(8)
    h = rng.permutation(N)
    full = h < N // 2
    nx, e = np.zeros((N, 8, P, 2), int), np.zeros((N, 8, T), int)
    for r in range(N):
        for g in range(8):
            nx[r, g] = rng.permutation(P)[:, None] if o[g] < 4 else rng.integers(0, 2, (P, 2)) * (P - 1)
            e[r, g] = rng.permutation(P)[:T] if full[r] else h[r] % 2 * (P - 1)
    return {**d, **chase(nx.reshape(N, 8, 2 * P), e)}
def setup_inputs_spread(rng):
    d = setup_inputs(rng)
    d["x"] = trim(wide(rng, N, 128, 4 * T, cols=6))
    d["k"] = trim(wide(rng, N, 128, 4 * P, cols=6))
    return d
def check_inputs(d):
    b = []
    for n in ("x", "k", "u", "v"):
        a = np.abs(d[n].astype(np.float32))
        if not (np.isfinite(a).all() and ((a == 0) | (a >= 2.0 ** -30) & (a <= 2.0 ** 30)).all()): b.append("a value of " + n)
    for n in ("nx", "st"):
        if ((d[n] < 0) | (d[n] >= P)).any(): b.append("an entry of " + n)
    if (d["wc"] != d["wc"][:1]).any(): b.append("wc differs between ranks")
    s = [mx_ref.live(p) for p in d["ws"]]
    if any((p != s[0]).any() for p in s): b.append("ws differs between ranks")
    return b
def reference(x, k, u, v, wc, ws, nx, st):
    w = pk(wc[0], ws[0])
    lay = [pick(w, np.arange(128 * b, 128 * b + 128)) for b in range(4)]
    qu = [mx_ref.quantize(u[r]) for r in range(N)]
    nodes = decode(join(*[mx_ref.quantize(k[r]) for r in range(N)])).astype(BF)
    now = [mx_ref.quantize(x[r]) for r in range(N)]
    p = [gentries(st[r]) for r in range(N)]
    for t in range(H):
        was = decode(join(*now))
        for r in range(N):
            m = (r + t) % N
            n = gcols(cut(nodes, m, 4 * P), p[r]).astype(np.float32)
            q = mx_ref.quantize(np.ascontiguousarray(((cut(was, r, 4 * T) + n) * np.float32(0.5)).astype(BF)))
            c = mx_ref.matmul(qu[m], q)[::16]
            p[r] = np.take_along_axis(nx[m], 2 * p[r] + (c > 0), axis=1)
            now[r] = mx_ref.quantize(tile([mx_ref.matmul(lay[b], q) * np.float32(0.03125) for b in range(4)]))
    y, pl = np.zeros((N, 128, T), np.float32), np.zeros((N, 8, T), np.float32)
    oc, osc = np.zeros((N, 128, 4 * T), np.uint8), np.zeros((N, 16, T), np.uint8)
    for r in range(N):
        y[r] = mx_ref.matmul(mx_ref.quantize(v[r]), now[r])
        pl[r] = p[r]
        oc[r], osc[r] = emit(now[r])
    return {"y": y, "pl": pl, "oc": oc, "osc": osc}

@@ -1,0 +1,322 @@
+from concourse.mybir import dt, AluOpType, ActivationFunctionType
+
+NT, NP, NH = 384, 480, 3
+CUT = 192
+TW = NP + 16
+MID = 240.0
+LOADS = ["ldk", "ldu", "ldx0", "ldw", "ldws", "ldx1"]
+CH = [(0, CUT), (CUT, NT)]
+NM = max(CUT, NT - CUT)
+X4, U8, BF, F32, I32, U16 = "float8_e4m3fn_x4", "uint8", "bfloat16", "float32", "int32", "uint16"
+
+SCRATCH = {"ps": ("psum", [128, 4096], F32)}
+_S = [("kt", 4 * NP, BF), ("xt", 4 * NT, BF), ("ut", 512, BF), ("vt", 512, BF), ("sti", 24, I32), ("et", 2048, BF),
+      ("jd", 128, BF), ("ident", 128, BF), ("pi", 1, I32), ("pa", 1, I32), ("pb", 1, I32), ("wa", 2 * NP, I32),
+      ("wb", 2 * NP, BF), ("nxi", 60, I32), ("nxb", 60, BF), ("j16", NM, BF), ("off", NM, BF), ("nxt", NM, BF),
+      ("wt", NM, BF), ("lui", 8, I32), ("lu", 8, U16), ("lc", 2, U16), ("l0", 96, U16), ("p0", 24, F32),
+      ("kg", 4 * NT, BF), ("yb", NT, F32), ("plb", NT, F32)]
+_S += [(_n, 1, F32) for _n in ("pm", "pm1", "me", "mo", "me2", "mo2", "e15", "rs", "iv", "bi")]
+_M = [("uu", 128), ("vv", 128), ("ww", 512), ("ea", 512), ("ee", 512), ("eo", 512), ("ng", NT), ("z0", NT)]
+for _t in range(NH):
+    _M += [("tb%d" % _t, TW), ("su%d" % _t, 128), ("bl%d" % _t, NT), ("z%d" % (_t + 1), NT)]
+    _S += [("bt%d" % _t, 4 * NT, BF), ("rt%d" % _t, 4 * NT, BF), ("bit%d" % _t, NT, BF), ("sa%d" % _t, NT, BF),
+           ("lf%d" % _t, 48, F32), ("ln%d" % _t, 48, U16)]
+    if _t > 0:
+        SCRATCH["nxd%d" % _t] = ("dram", [128, 60], BF)
+        _M += [("pk%d" % _t, 2 * NT)]
+        _S += [("gm%d" % _t, 2 * NT, BF), ("sb%d" % _t, 2 * NT, BF), ("xa%d" % _t, 48, F32), ("lp%d" % _t, 48, U16), ("p%d" % _t, 24, F32)]
+for _n, _c in _M:
+    _S += [(_n + "q", _c, X4), (_n + "s", _c, U8)]
+for _n, _c, _d in _S:
+    SCRATCH[_n] = ("sbuf", [128, _c], _d)
+
+ADD, MUL, EQ = AluOpType.add, AluOpType.mult, AluOpType.is_equal
+COPY, IDENT = ActivationFunctionType.Copy, ActivationFunctionType.Identity
+
+
+def build(T, topo, core):
+    ops, cur = [], [None]
+
+    def op(name, eng, cost, fn, R=(), W=(), kind="c", after=(), arr=(), grp=None):
+        ops.append({"name": name, "eng": eng, "cost": cost, "fn": fn, "R": list(R), "W": list(W), "kind": kind,
+                    "after": list(after), "arr": list(arr), "grp": grp, "half": cur[0]})
+        return name
+
+    def B(n, a, b, s=1):
+        return T[n][:, a:b:s] if s != 1 else T[n][:, a:b]
+
+    def u8(n, a, b):
+        return T[n][:, a:b].bitcast(dt.uint8)
+
+    def dma(name, eng, pair, nbytes, rows, R, W, after=(), arr=()):
+        return op(name, eng, ("dma", nbytes, rows), lambda e, q: q.dma_start(*pair()), R, W, "dma", after, arr)
+
+    def peer(t):
+        return T.cores[(T.rank_of(core) - t) % len(T.cores)]
+
+    def val(v):
+        return T[v][:] if isinstance(v, str) and v in SCRATCH else v
+
+    def affine(out, src, s, c=None):
+        def fn(e, q):
+            if e == "V":
+                return q.tensor_scalar(out(), src(), val(s), None, MUL) if c is None else q.tensor_scalar(out(), src(), val(s), val(c), MUL, ADD)
+            if isinstance(s, str) or c is not None:
+                return q.activation(out(), src(), IDENT, bias=0.0 if c is None else val(c), scale=val(s))
+            return q.activation(out(), src(), COPY, scale=s)
+        return fn
+
+    def moved(out, src):
+        return lambda e, q: q.tensor_copy(out(), src()) if e == "V" else q.activation(out(), src(), COPY)
+
+    def quant(name, dst, a, b, src, s0):
+        s1 = s0 + 4 * (b - a)
+        op(name, "V", ("q", s1 - s0), lambda e, q: q.quantize_mx(B(dst + "q", a, b), B(dst + "s", a, b), B(src, s0, s1)),
+           [(src, s0, s1)], [(dst + "q", a, b), (dst + "s", a, b)])
+
+    def pick(name, dst, a, b, src, w0, w1, lst, l0, arr=()):
+        l1 = l0 + (b - a) // 16
+        op(name + "q", "V", ("g", b - a),
+           lambda e, q: q.tensor_copy(B(dst + "q", a, b).bitcast(dt.uint32),
+                                      B(src + "q", w0, w1).bitcast(dt.uint32).indirect(B(lst, l0, l1))),
+           [(src + "q", w0, w1), (lst, l0, l1)], [(dst + "q", a, b)], arr=arr)
+        op(name + "s", "VS", ("g", b - a),
+           moved(lambda: B(dst + "s", a, b), lambda: B(src + "s", w0, w1).indirect(B(lst, l0, l1))),
+           [(src + "s", w0, w1), (lst, l0, l1)], [(dst + "s", a, b)], arr=arr)
+
+    def mm(name, bank, st, s0, mv, a, b, start, stop, grp=None):
+        op(name, "P", ("p", b - a),
+           lambda e, q: q.matmul_mx(B("ps", 512 * bank, 512 * bank + b - a), B(st + "q", s0, s0 + 128),
+                                    B(st + "s", s0, s0 + 128), B(mv + "q", a, b), B(mv + "s", a, b), start, stop),
+           [(st + "q", s0, s0 + 128), (st + "s", s0, s0 + 128), (mv + "q", a, b), (mv + "s", a, b)],
+           [("ps", bank, bank + 1)], grp=grp)
+
+    def vec(name, fn, R, W, n=1, f=1.0):
+        op(name, "V", ("e", n * f), fn, R, W)
+
+    def fill(buf, eng, after):
+        for h in range(4):
+            a, b = 240 * h, 240 * h + 240
+            op("fill%s%d" % (buf, h), eng, ("fill", 240),
+               lambda e, q, a=a, b=b: q.memset(B(buf, a, b), 0) if e == "V"
+               else q.iota(B(buf, a, b), [[0, 240]], 0, 0, allow_small_or_imprecise_dtypes=buf == "wb"), [], [(buf, a, b)], after=after)
+
+    kids = [("wa", 0), ("wb", 0), ("wb", 1)]
+
+    def rows(t, after, arr):
+        buf, r = kids[t]
+        return [dma("rows%d" % t, "Y", lambda: (T[buf][r:128:16, :], T["nxd%d" % t][:] if t else T.nx[:]), 30720, 16,
+                    [], [(buf, 0, 2 * NP, r)], after, arr)]
+
+    l = dma("ldnx", "S", lambda: (T.nxi[:], T.nx[:]), 30720, 128, [], [("nxi", 0, 60)])
+    dma("ldst", "S", lambda: (T.sti[:], T.st[:]), 12288, 128, [], [("sti", 0, 24)], [l])
+    loads = {"ldk": ("kt", "k", 0, 4 * NP), "ldu": ("ut", "u", 0, 512),
+             "ldx0": ("xt", "x", 0, 4 * CUT), "ldx1": ("xt", "x", 4 * CUT, 4 * NT)}
+    l = []
+    for name in LOADS:
+        if name in loads:
+            d, s, a, b = loads[name]
+            l = [dma(name, "Y", lambda d=d, s=s, a=a, b=b: (B(d, a, b), B(s, a, b)), 256 * (b - a), 128, [], [(d, a, b)], l)]
+        elif name == "ldw":
+            l = [dma(name, "Y", lambda: (u8("wwq", 0, 512), T.wc[:]), 262144, 128, [], [("wwq", 0, 512)], l)]
+        else:
+            l = [dma(name, "Y", lambda: (T.wws[:], T.ws[:]), 65536, 128, [], [("wws", 0, 512)], l)]
+
+    for name, pat, cm, n, prev in [("jd", [[1, 128]], -1, 128, []), ("pi", [[0, 1]], 1, 1, ["iojd"]), ("lui", [[2, 8]], 0, 8, ["iopi"]),
+                                   ("j16", [[0, NM // 16], [1, 16]], 0, NM, ["iolui"])]:
+        op("io" + name, "G", ("io", n),
+           lambda e, q, name=name, pat=pat, cm=cm: q.iota(T[name][:], pat, 0, cm, allow_small_or_imprecise_dtypes=name[0] == "j"),
+           [], [(name, 0, n)], after=prev)
+    fill("wa", "VG", ["ioj16"])
+    for h in range(2):
+        vec("zero%d" % h, lambda e, q, h=h: q.memset(B("et", 1024 * h, 1024 * h + 1024), 0.0), [],
+            [("et", 1024 * h, 1024 * h + 1024)], 1024, 0.5)
+    for name, src, n, args in [
+            ("ident", "jd", 128, (0.0, None, EQ)), ("pa", "pi", 1, (4, 1, AluOpType.logical_shift_right, AluOpType.bitwise_and)),
+            ("pb", "pi", 1, (15, None, AluOpType.bitwise_and)), ("me", "pa", 1, (0.0, None, EQ)), ("mo", "pa", 1, (1.0, None, EQ)),
+            ("nxb", "nxi", 60, (-MID, None, ADD)), ("e15", "pb", 1, (15.0, None, EQ)), ("rs", "e15", 1, (31.0 / 64, 1.0 / 64, MUL, ADD)),
+            ("iv", "e15", 1, (-124.0, 128.0, MUL, ADD)), ("bi", "iv", 1, (MID, None, MUL)), ("me2", "pa", 1, (0.0, "iv", EQ, MUL)),
+            ("mo2", "pa", 1, (1.0, "iv", EQ, MUL)), ("pm1", "pb", 1, (1.0, None, ADD)), ("pm", "pb", 1, (1.0, None, MUL)),
+            ("lc", "pb", 1, (8.0, None, MUL)), ("lu", "lui", 8, (1.0, None, MUL)), ("off", "j16", NM, ("pm", None, AluOpType.not_equal)),
+            ("nxt", "j16", NM, ("pm1", 31.0, EQ, MUL)), ("p0", "sti", 24, ("iv", None, MUL))]:
+        vec(name, lambda e, q, name=name, src=src, n=n, args=args: q.tensor_scalar(B(name, 0, n), B(src, 0, n), *[val(v) for v in args]),
+            [(src, 0, n)] + [(v, 0, 1) for v in args if isinstance(v, str) and v in SCRATCH], [(name, 0, n)], n, 0.5)
+    vec("wt", lambda e, q: q.tensor_tensor(T.wt[:], T.off[:], T.nxt[:], ADD), [("off", 0, NM), ("nxt", 0, NM)], [("wt", 0, NM)], NM, 2)
+    for name, mask in [("ea", None), ("ee", "me"), ("eo", "mo")]:
+        for h in range(2):
+            for b in (2 * h, 2 * h + 1):
+                out, src = (lambda b=b: B("et", 513 * b, 512 * b + 512, 4)), (lambda: T.ident[:])
+                op("d%s%d" % (name, b), "VS", ("e", 128), affine(out, src, mask) if mask else moved(out, src),
+                   [("ident", 0, 128)] + ([(mask, 0, 1)] if mask else []), [("et", 512 * b, 512 * b + 512)])
+            quant("q%s%d" % (name, h), name, 256 * h, 256 * h + 256, "et", 1024 * h)
+    l = rows(0, l, [])
+
+    def send_nx(t, after):
+        def fn(e, q):
+            rid, pid = topo.addr(peer(t))[:2]
+            return q.remote_dma(T["nxd%d" % t][:], T.nxb[:], T.sem["anx%d" % t], T.sem.sent, pid, rid, topo.mask(core, peer(t)))
+        op("sn%d" % t, "G", ("rem", 15360, 128), fn, [("nxb", 0, 60)], [], "rem", after)
+    send_nx(1, ["ioj16"])
+
+    def send(name, t, kind, a, b, after, arr=()):
+        def fn(e, q):
+            rid, pid = topo.addr(peer(t))[:2]
+            view = u8 if kind == "q" else B
+            return q.remote_dma(view("tb%d%s" % (t, kind), a, b), view("tb0" + kind, a, b), T.sem["atb%d" % t], T.sem.sent,
+                                pid, rid, topo.mask(core, peer(t)))
+        op(name, "G", ("rem", (512 if kind == "q" else 128) * (b - a), 128), fn, [("tb0" + kind, a, b)], [], "rem", after, arr)
+
+    quant("qk", "tb0", 0, NP, "kt", 0)
+    quant("qu", "uu", 0, 128, "ut", 0)
+    pick("pku", "tb0", NP, TW, "uu", 0, 128, "lc", 0)
+    send("s1b", 1, "q", 0, TW, ["sn1"])
+    send("s1s", 1, "s", 0, TW, ["s1b"])
+    fill("wb", "G", ["s1s"])
+    l = rows(1, l, ["anx1"])
+    send("s2c", 2, "q", 0, TW, l, ["anx1"])
+    send("s2s", 2, "s", 0, TW, ["s2c"])
+    send_nx(2, ["s2s"])
+    dma("ldv", "Y", lambda: (T.vt[:], T.v[:]), 131072, 128, [], [("vt", 0, 512)], l, ["atb1"])
+    quant("qv", "vv", 0, 128, "vt", 0)
+    for t in range(4):
+        vec("l0%d" % t, lambda e, q, t=t: q.tensor_scalar(B("l0", 24 * t, 24 * t + 24), T.sti[:], 4.0, float(t), MUL, ADD),
+            [("sti", 0, 24)], [("l0", 24 * t, 24 * t + 24)])
+
+    def hop(t, c):
+        a, b = CH[c]
+        n, la, lb, k0 = b - a, a // 16, b // 16, 4 * c
+        tag, arr = "%d%d" % (t, c), (["atb%d" % t] if t else [])
+        z, zn, bl, bt, rt = "z%d" % t, "z%d" % (t + 1), "bl%d" % t, "bt%d" % t, "rt%d" % t
+
+        def bank(i):
+            return B("ps", 512 * (k0 + i), 512 * (k0 + i) + n)
+        if t == 0:
+            for i in range(4):
+                op("kg%d%d" % (c, i), "VS", ("g", n),
+                   moved(lambda i=i: B("kg", 4 * a + i, 4 * b, 4), lambda i=i: T.kt[:].indirect(B("l0", 24 * i + la, 24 * i + lb))),
+                   [("kt", 0, 4 * NP), ("l0", 24 * i + la, 24 * i + lb)], [("kg", 4 * a, 4 * b, i)])
+            quant("qg%d" % c, "ng", a, b, "kg", 4 * a)
+            quant("qx%d" % c, "z0", a, b, "xt", 4 * a)
+            terms = [("ea", "ng", a), ("ea", "z0", a)]
+        else:
+            pick("pe" + tag, "pk%d" % t, 2 * a, 2 * b, "tb%d" % t, 0, NP, "lp%d" % t, 2 * la, arr)
+            terms = [("ea", z, a), ("ee", "pk%d" % t, 2 * a), ("eo", "pk%d" % t, a + b)]
+        for j, (st, mv, m0) in enumerate(terms):
+            for i in range(4):
+                mm("mb%s%d%d" % (tag, j, i), k0 + i, st, 128 * i, mv, m0, m0 + n, j == 0, j == len(terms) - 1, grp="b%s%d" % (tag, i))
+        for i in range(4):
+            op("eb%s%d" % (tag, i), "VS", ("e", n), affine(lambda i=i: B(bt, 4 * a + i, 4 * b, 4), lambda i=i: bank(i), 0.5),
+               [], [("ps", k0 + i, k0 + i + 1), (bt, 4 * a, 4 * b, i)])
+        quant("qb" + tag, bl, a, b, bt, 4 * a)
+        mm("ms" + tag, k0, "su%d" % t, 0, bl, a, b, True, True)
+        bit, sa, lf, ln, pn, (win, row) = "bit%d" % t, "sa%d" % t, "lf%d" % t, "ln%d" % t, "p%d" % t, kids[t]
+        op("gt" + tag, "S", ("e", n), lambda e, q: q.activation(B(bit, a, b), bank(0), ActivationFunctionType.Sign, bias=-2.0 ** -120),
+           [], [("ps", k0, k0 + 1), (bit, a, b)])
+        vec("sa" + tag, lambda e, q: q.tensor_tensor_scan(B(sa, a, b), B("wt", 0, n), B(bit, a, b), 0.0, MUL, ADD),
+            [("wt", 0, n), (bit, a, b)], [(sa, a, b)], n, 0.5)
+        rep = 2 if t < NH - 1 else 1
+        f0, f1 = 2 * la, 2 * la + rep * (lb - la)
+        for r in range(rep):
+            vec("lf%s%d" % (tag, r), lambda e, q, r=r: q.tensor_tensor(B(lf, f0 + r, f1, rep), B(sa, a + 15, b, 16), B(pn, la, lb), ADD),
+                [(sa, a, b), (pn, la, lb)], [(lf, f0, f1, r)])
+        vec("ln" + tag, lambda e, q: q.tensor_scalar(B(ln, f0, f1), B(lf, f0, f1), T.rs[:], 0.74, MUL, ADD),
+            [(lf, f0, f1), ("rs", 0, 1)], [(ln, f0, f1)])
+        if t == NH - 1:
+            op("pl" + tag, "VS", ("g", n), affine(lambda: B("plb", a, b), lambda: T[win][:].indirect(B(ln, f0, f1)), 1.0, MID),
+               [(win, 0, 2 * NP), (ln, f0, f1)], [("plb", a, b)])
+        else:
+            gm, sb, xa, lp, p2 = ["%s%d" % (s, t + 1) for s in ("gm", "sb", "xa", "lp", "p")]
+            op("gm" + tag, "VS" if t else "V", ("g", 2 * n),
+               affine(lambda: B(gm, 2 * a, 2 * b), lambda: T[win][:].indirect(B(ln, f0, f1)), 1.0, None if t else -MID),
+               [(win, 0, 2 * NP), (ln, f0, f1)], [(gm, 2 * a, 2 * b)])
+            vec("sb" + tag, lambda e, q: q.transpose(B(sb, 2 * a, 2 * b), B(gm, 2 * a, 2 * b)),
+                [(gm, 2 * a, 2 * b)], [(sb, 2 * a, 2 * b)], 2 * n, 0.5)
+            for h, m in enumerate(("me2", "mo2")):
+                x0, x1, src = 2 * la + h * (lb - la), la + lb + h * (lb - la), (lambda h=h: B(sb, 2 * a + 16 * h + row, 2 * b, 32))
+                vec("lp%s%d" % (tag, h), lambda e, q, x0=x0, x1=x1, src=src: q.tensor_scalar(B(lp, x0, x1), src(), MID, None, ADD),
+                    [(sb, 2 * a, 2 * b)], [(lp, x0, x1)])
+                op("ph%s%d" % (tag, h), "VS", ("e", 1), affine(lambda x0=x0, x1=x1: B(xa, x0, x1), src, m, None if h else "bi"),
+                   [(sb, 2 * a, 2 * b), (m, 0, 1), ("bi", 0, 1)], [(xa, x0, x1)])
+            vec("p2" + tag, lambda e, q: q.tensor_tensor(B(p2, la, lb), B(xa, 2 * la, la + lb), B(xa, la + lb, 2 * lb), ADD),
+                [(xa, 2 * la, 2 * lb)], [(p2, la, lb)])
+        for i in (1, 2, 3, 0):
+            mm("mr%s%d" % (tag, i), k0 + i, "ww", 128 * i, bl, a, b, True, True)
+            op("er%s%d" % (tag, i), "VS", ("e", n), affine(lambda i=i: B(rt, 4 * a + i, 4 * b, 4), lambda i=i: bank(i), 0.03125),
+               [], [("ps", k0 + i, k0 + i + 1), (rt, 4 * a, 4 * b, i)])
+        quant("qz" + tag, zn, a, b, rt, 4 * a)
+        if t == NH - 1:
+            mm("my%d" % c, k0 + 1, "vv", 0, zn, a, b, True, True)
+            op("ey%d" % c, "VS", ("e", n), moved(lambda: B("yb", a, b), lambda: bank(1)), [], [("ps", k0 + 1, k0 + 2), ("yb", a, b)])
+            dma("sty%d" % c, "YS", lambda: (B("y", a, b), B("yb", a, b)), 512 * n, 128, [("yb", a, b)], [])
+            dma("stc%d" % c, "YS", lambda: (B("oc", 4 * a, 4 * b), u8(zn + "q", a, b)), 512 * n, 128, [(zn + "q", a, b)], [])
+
+    for t in range(NH):
+        pick("su%d" % t, "su%d" % t, 0, 128, "tb%d" % t, NP, TW, "lu", 0, ["atb%d" % t] if t else [])
+        if t == 2:
+            rows(2, ["ldv"], ["anx2"])
+        for c in range(2):
+            cur[0] = c
+            hop(t, c)
+            cur[0] = None
+    for k in range(4):
+        dma("sts%d" % k, "YS", lambda k=k: (T.osc[4 * k:4 * k + 4, :], T.z3s[32 * k:32 * k + 4, :]), 1536, 4, [("z3s", 0, NT)], [])
+    dma("stp", "YS", lambda: (T.pl[:], T.plb[kids[2][1]:128:16, :]), 12288, 16, [("plb", 0, NT)], [])
+    return ops
+
+
+ARR = {"anx1": (["sn1"], 1, 1), "anx2": (["sn2"], 2, 1), "atb1": (["s1b", "s1s"], 1, 2), "atb2": (["s2c", "s2s"], 2, 2)}
+
+
+def overlap(r, s):
+    if r[0] != s[0] or r[2] <= s[1] or s[2] <= r[1]:
+        return False
+    return len(r) < 4 or len(s) < 4 or r[3] == s[3]
+
+
+def link(ops):
+    for i, o in enumerate(ops):
+        o["dep"] = [j for j, p in enumerate(ops[:i]) if (o["grp"] is None or o["grp"] != p["grp"]) and (
+            any(overlap(r, s) for r in o["R"] + o["W"] for s in p["W"]) or any(overlap(r, s) for r in o["W"] for s in p["R"]))]
+    return ops
+
+
+ORDER = """
+2Y 0S 8G 3Y 1S 4Y 5Y 6Y 9G 7Y 18V 10G 17V 11G 33V 20V 12G 31V 16V 15G 30V 39S 38V 41S 42V 40V 13G 24V 19V 14G 56Y 23V 32V 57G 34V 26V 35V 59V 76V 74V 82S 75V 60V 77V 58V 81S 83S 80V 62G 121S 43V 21V 122S 25V 84V 124S 123V 88P 86P 89P 22V 61S 85V 45S 63G 44S 37V 92P 87P 66G 96S 91P 36V 90P 125V 95S 93P 126V 97S 128P 64G 129P 94V 79S 130P 78V 132P 47S 133P 98V 48S 134P 65G 136S 46V 99P 127P 100S 27V 131P 49V 116P 137S 67G 114P 101V 118P 135S 29V 102V 138S 103V 28V 104V 119S 68Y 69G 139V 50S 105V 53S 140P 70G 112P 115S 155P 141S 71G 117S 142V 159P 106V 157P 113S 153P 144V 54S 143V 156S 109V 107V 145V 154S 120V 158S 146V 167P 110S 166P 160S 168P 169P 51S 161V 165S 72Y 147V 207P 210P 164V 208P 209P 163S 149S 148V 170P 150V 55V 171P 206S 172P 52V 173P 176P 177P 205V 175P 180S 174P 181S 178S 179V 213P 108S 212P 162V 216P 182V 217P 220S 211P 151V 183P 111V 221V 215P 184S 198P 152V 214P 219V 199S 202P 185V 218P 203S 196P 186V 200P 187V 222S 188V 197V 189S 223V 201V 224P 239P 225S 204V 240S 190V 243P 241P 247S 226V 254P 193V 191V 237P 227V 253P 250S 228V 249V 252P 251P 244S 229V 255P 242V 230S 257P 238V 256P 259P 246V 261P 260P 245V 263S 258P 248Y 262P 231V 264S 291P 265V 292P 266S 290P 232V 233S 289P 234V 192S 267V 288S 287V 268P 278P 276P 274P 269S 277V 296P 275S 293P 194V 279V 235S 280P 295P 270V 281S 297P 73V 294P 301S 282V 300P 298P 304S 236V 299P 302V 283P 303S 195V 284S 305V 286S 285S 306P 312P 307S 316P 313V 314P 317S 318P 315V 319S 308V 271V 320V 309V 327Y 324S 321P 272V 326Y 325S 310V 328S 322V 273S 311V 323Y 329Y
+"""
+_OPS = build(None, None, None)
+PLAN = [(int(w[:-1]), w[-1]) for w in ORDER.split()]
+SEMAPHORES = ["cV", "cS", "cP", "cG", "sent"] + sorted(ARR) + ["d" + o["name"] for o in _OPS if o["kind"] == "dma"]
+
+
+def rank_program(g, core, T, topo):
+    rank, n = T.rank_of(core), len(T.cores)
+    if rank is None:
+        return
+    ops = link(build(T, topo, core))
+    arrive = {a: ARR[a][2] * len(topo.engines(T.cores[(rank + ARR[a][1]) % n], core)) for a in ARR}
+    queue = {"V": g.vector, "S": g.scalar, "P": g.tensor, "G": g, "Y": g.sync}
+    known = {e: {} for e in queue}
+    count, event = dict(arrive), {}
+    for i, e in PLAN:
+        o, q, kn = ops[i], queue[e], known[e]
+        top = {}
+        for s, v, clock in [event[j] for j in o["dep"]] + [(a, arrive[a], {}) for a in o["arr"]]:
+            if v > top.get(s, (0, None))[0]:
+                top[s] = (v, clock)
+        for s in sorted(top, key=lambda s: -len(top[s][1])):
+            v, clock = top[s]
+            if kn.get(s, 0) < v:
+                q.wait_ge(T.sem[s], v)
+                kn[s] = v
+                for s2, v2 in clock.items():
+                    kn[s2] = max(kn.get(s2, 0), v2)
+        ins = o["fn"](e, q)
+        if o["kind"] == "rem":
+            s, inc = "sent", len(topo.engines(core, T.cores[(rank - int(o["name"].replace("n", "")[1])) % n]))
+        else:
+            s, inc = ("c" + e, 1) if o["kind"] == "c" else ("d" + o["name"], 16)
+            ins.then_inc(T.sem[s], inc)
+        count[s] = count.get(s, 0) + inc
+        event[i] = (s, count[s], dict(kn))
+    for s in sorted(count):
+        g.wait_ge(T.sem[s], count[s])

@@ -108,11 +108,11 @@ def build(T, topo, core):
         return [dma("rows%d" % t, "Y", lambda: (T[buf][r:128:16, :], T["nxd%d" % t][:] if t else T.nx[:]), 30720, 16,
                     [], [(buf, 0, 2 * NP, r)], after, arr)]
 
-    l = dma("ldnx", "S", lambda: (T.nxi[:], T.nx[:]), 30720, 128, [], [("nxi", 0, 60)])
-    dma("ldst", "S", lambda: (T.sti[:], T.st[:]), 12288, 128, [], [("sti", 0, 24)], [l])
+    l = dma("ldst", "Y", lambda: (T.sti[:], T.st[:]), 12288, 128, [], [("sti", 0, 24)])
+    dma("ldnx", "S", lambda: (T.nxi[:], T.nx[:]), 30720, 128, [], [("nxi", 0, 60)], [l])
     loads = {"ldk": ("kt", "k", 0, 4 * NP), "ldu": ("ut", "u", 0, 512),
              "ldx0": ("xt", "x", 0, 4 * CUT), "ldx1": ("xt", "x", 4 * CUT, 4 * NT)}
-    l = []
+    l = ["ldnx"]
     for name in LOADS:
         if name in loads:
             d, s, a, b = loads[name]
@@ -169,7 +169,7 @@ def build(T, topo, core):
     quant("qk", "tb0", 0, NP, "kt", 0)
     quant("qu", "uu", 0, 128, "ut", 0)
     pick("pku", "tb0", NP, TW, "uu", 0, 128, "lc", 0)
-    send("s1b", 1, "q", 0, TW, ["sn1"])
+    send("s1b", 1, "q", 0, TW, ["sn1", "rows0"])
     send("s1s", 1, "s", 0, TW, ["s1b"])
     fill("wb", "G", ["s1s"])
     l = rows(1, l, ["anx1"])
@@ -281,7 +281,7 @@ def link(ops):
 
 
 ORDER = """
-2Y 0S 8G 3Y 1S 4Y 5Y 6Y 9G 7Y 18V 10G 17V 11G 33V 20V 12G 31V 16V 15G 30V 39S 38V 41S 42V 40V 13G 24V 19V 14G 56Y 23V 32V 57G 34V 26V 35V 59V 76V 74V 82S 75V 60V 77V 58V 81S 83S 80V 62G 121S 43V 21V 122S 25V 84V 124S 123V 88P 86P 89P 22V 61S 85V 45S 63G 44S 37V 92P 87P 66G 96S 91P 36V 90P 125V 95S 93P 126V 97S 128P 64G 129P 94V 79S 130P 78V 132P 47S 133P 98V 48S 134P 65G 136S 46V 99P 127P 100S 27V 131P 49V 116P 137S 67G 114P 101V 118P 135S 29V 102V 138S 103V 28V 104V 119S 68Y 69G 139V 50S 105V 53S 140P 70G 112P 115S 155P 141S 71G 117S 142V 159P 106V 157P 113S 153P 144V 54S 143V 156S 109V 107V 145V 154S 120V 158S 146V 167P 110S 166P 160S 168P 169P 51S 161V 165S 72Y 147V 207P 210P 164V 208P 209P 163S 149S 148V 170P 150V 55V 171P 206S 172P 52V 173P 176P 177P 205V 175P 180S 174P 181S 178S 179V 213P 108S 212P 162V 216P 182V 217P 220S 211P 151V 183P 111V 221V 215P 184S 198P 152V 214P 219V 199S 202P 185V 218P 203S 196P 186V 200P 187V 222S 188V 197V 189S 223V 201V 224P 239P 225S 204V 240S 190V 243P 241P 247S 226V 254P 193V 191V 237P 227V 253P 250S 228V 249V 252P 251P 244S 229V 255P 242V 230S 257P 238V 256P 259P 246V 261P 260P 245V 263S 258P 248Y 262P 231V 264S 291P 265V 292P 266S 290P 232V 233S 289P 234V 192S 267V 288S 287V 268P 278P 276P 274P 269S 277V 296P 275S 293P 194V 279V 235S 280P 295P 270V 281S 297P 73V 294P 301S 282V 300P 298P 304S 236V 299P 302V 283P 303S 195V 284S 305V 286S 285S 306P 312P 307S 316P 313V 314P 317S 318P 315V 319S 308V 271V 320V 309V 327Y 324S 321P 272V 326Y 325S 310V 328S 322V 273S 311V 323Y 329Y
+16V 0Y 1S 8G 2Y 3Y 4Y 5Y 9G 6Y 7Y 10G 18V 19V 11G 38S 20V 17V 39S 14G 40V 41S 42S 24V 21V 33V 13G 45S 26V 44S 75V 77V 43V 15G 30V 47S 46V 48S 23V 76V 12G 22V 49V 51S 74V 57G 56Y 58V 82S 80S 32V 59V 83S 81V 122S 60V 31V 61V 84V 121S 62G 85V 87P 88P 124S 123V 92P 63G 86P 27V 96S 90P 35V 91P 78V 66G 94S 89P 93P 95S 25V 125V 97S 36V 64G 127P 34V 79S 129P 128P 50S 65G 126V 98V 133P 37V 137S 99P 67G 131P 100S 132P 52V 130P 54S 134P 136S 101V 116P 68Y 69G 53V 114P 135S 112P 102V 103V 138S 118P 70G 55V 117S 104V 139V 115S 71G 119S 105V 140P 157P 141S 153P 154S 159P 142V 155P 106V 113S 144V 156S 143V 107V 160S 109V 145V 120V 158S 146V 169P 166P 167P 168P 161V 147V 207P 208P 209P 164V 163S 72Y 210P 165S 148V 150V 28V 205V 206S 173P 172P 176P 170P 174P 29V 180S 177P 171P 178S 175P 181S 214P 179V 218P 211P 162V 222S 213P 215P 110V 151S 108V 217P 182V 212P 221S 216P 183P 219S 220V 198P 200P 184S 111V 223V 196P 199S 185V 224P 149S 201V 197S 202P 186V 239P 225S 187V 241P 152V 188V 203S 243P 226V 237P 189S 227V 228V 204V 229V 251P 230S 252P 190V 254P 253P 191V 193V 238V 250S 248Y 249V 244S 231V 256P 242S 258P 240V 233S 255P 192S 232V 260P 235S 234V 259P 245V 288S 262P 287V 257P 291P 261P 290P 194S 292P 263S 264V 289P 296P 265S 246V 300P 266S 294P 73V 298P 247S 295P 267V 299P 302S 293P 195V 304V 297P 303S 268P 301V 278P 269S 276P 236V 274P 305V 277S 280P 279V 275S 306P 316P 281V 307S 314P 270V 312P 315S 282V 318P 313S 317V 286Y 283P 319V 284S 308V 320V 285S 309V 326Y 321P 271V 324Y 310V 328Y 272V 325Y 311S 322V 327Y 273V 323Y 329Y
 """
 _OPS = build(None, None, None)
 PLAN = [(int(w[:-1]), w[-1]) for w in ORDER.split()]

@@ -1,30 +1,31 @@
+from concourse.bass import DstId, RemoteDMATransfer
 from concourse.mybir import dt, AluOpType, ActivationFunctionType
 
 NT, NP, NH = 384, 480, 3
 CUT = 192
-TW = NP + 16
+TW = NP + 128
 MID = 240.0
-LOADS = ["ldk", "ldu", "ldx0", "ldw", "ldws", "ldx1"]
+LOADS = ["ldst", "ldk", "ldx0", "ldx1", "ldu", "ldw", "ldws"]
 CH = [(0, CUT), (CUT, NT)]
-NM = max(CUT, NT - CUT)
+NM = max(CUT, NT - CUT) // 16
 X4, U8, BF, F32, I32, U16 = "float8_e4m3fn_x4", "uint8", "bfloat16", "float32", "int32", "uint16"
 
-SCRATCH = {"ps": ("psum", [128, 4096], F32)}
-_S = [("kt", 4 * NP, BF), ("xt", 4 * NT, BF), ("ut", 512, BF), ("vt", 512, BF), ("sti", 24, I32), ("et", 2048, BF),
-      ("jd", 128, BF), ("ident", 128, BF), ("pi", 1, I32), ("pa", 1, I32), ("pb", 1, I32), ("wa", 2 * NP, I32),
-      ("wb", 2 * NP, BF), ("nxi", 60, I32), ("nxb", 60, BF), ("j16", NM, BF), ("off", NM, BF), ("nxt", NM, BF),
-      ("wt", NM, BF), ("lui", 8, I32), ("lu", 8, U16), ("lc", 2, U16), ("l0", 96, U16), ("p0", 24, F32),
-      ("kg", 4 * NT, BF), ("yb", NT, F32), ("plb", NT, F32)]
-_S += [(_n, 1, F32) for _n in ("pm", "pm1", "me", "mo", "me2", "mo2", "e15", "rs", "iv", "bi")]
-_M = [("uu", 128), ("vv", 128), ("ww", 512), ("ea", 512), ("ee", 512), ("eo", 512), ("ng", NT), ("z0", NT)]
+SCRATCH = {"ps": ("psum", [128, 4096], F32), "nxh": ("dram", [128, 60], BF)}
+_S = [("kt", 4 * NP, BF), ("xt", 4 * NT, BF), ("ut", 512, BF), ("vt", 512, BF), ("sti", 24, I32),
+      ("jd", 128, BF), ("za", 516, BF), ("ze", 516, BF), ("zo", 516, BF), ("pi", 1, I32), ("pa", 1, I32), ("pb", 1, I32),
+      ("wb", 2 * NP, BF), ("nxi", 60, I32), ("nxb", 60, BF), ("lu", 8, U16), ("l0", 96, U16),
+      ("kg", 4 * NT, BF), ("yb", NT, F32), ("plb", NT, F32), ("dd", 2 * NM, F32)]
+_S += [(_n, 1, F32) for _n in ("pm", "pm1", "me", "mo", "dc", "c0", "cl")]
+_S += [(_n, 16 * NM, BF) for _n in ("jr", "off", "nxt", "wt")]
+_M = [("uu", 128), ("vv", 128), ("ww", 512), ("ea", 512), ("ee", 512), ("eo", 512), ("ng", NT), ("z0", NT), ("tbh", TW)]
 for _t in range(NH):
-    _M += [("tb%d" % _t, TW), ("su%d" % _t, 128), ("bl%d" % _t, NT), ("z%d" % (_t + 1), NT)]
-    _S += [("bt%d" % _t, 4 * NT, BF), ("rt%d" % _t, 4 * NT, BF), ("bit%d" % _t, NT, BF), ("sa%d" % _t, NT, BF),
-           ("lf%d" % _t, 48, F32), ("ln%d" % _t, 48, U16)]
+    _M += [("tb%d" % _t, TW), ("bl%d" % _t, NT), ("z%d" % (_t + 1), NT)]
+    _S += [("bt%d" % _t, 4 * NT, BF), ("rt%d" % _t, 4 * NT, BF), ("ln%d" % _t, 48, U16),
+           ("bit%d" % _t, NT, BF), ("sa%d" % _t, NT, BF), ("lf%d" % _t, 48, F32), ("pn%d" % _t, 48, F32)]
     if _t > 0:
         SCRATCH["nxd%d" % _t] = ("dram", [128, 60], BF)
         _M += [("pk%d" % _t, 2 * NT)]
-        _S += [("gm%d" % _t, 2 * NT, BF), ("sb%d" % _t, 2 * NT, BF), ("xa%d" % _t, 48, F32), ("lp%d" % _t, 48, U16), ("p%d" % _t, 24, F32)]
+        _S += [("gm%d" % _t, 2 * NT, BF), ("sb%d" % _t, 2 * NT, BF), ("lp%d" % _t, 48, U16)]
 for _n, _c in _M:
     _S += [(_n + "q", _c, X4), (_n + "s", _c, U8)]
 for _n, _c, _d in _S:
@@ -34,12 +35,17 @@ ADD, MUL, EQ = AluOpType.add, AluOpType.mult, AluOpType.is_equal
 COPY, IDENT = ActivationFunctionType.Copy, ActivationFunctionType.Identity
 
 
-def build(T, topo, core):
-    ops, cur = [], [None]
+def helper(T, topo, rank):
+    core, to = T.cores[rank], T.cores[(rank - 2) % len(T.cores)]
+    return [c for c in topo.cores_of(core) if topo.die(c) != topo.die(core) and T.rank_of(c) is None and topo.may_write(c, to)][0]
+
+
+def build(T, topo, rank):
+    ops = []
 
     def op(name, eng, cost, fn, R=(), W=(), kind="c", after=(), arr=(), grp=None):
         ops.append({"name": name, "eng": eng, "cost": cost, "fn": fn, "R": list(R), "W": list(W), "kind": kind,
-                    "after": list(after), "arr": list(arr), "grp": grp, "half": cur[0]})
+                    "after": list(after), "arr": list(arr), "grp": grp})
         return name
 
     def B(n, a, b, s=1):
@@ -52,7 +58,7 @@ def build(T, topo, core):
         return op(name, eng, ("dma", nbytes, rows), lambda e, q: q.dma_start(*pair()), R, W, "dma", after, arr)
 
     def peer(t):
-        return T.cores[(T.rank_of(core) - t) % len(T.cores)]
+        return T.cores[(rank - t) % len(T.cores)]
 
     def val(v):
         return T[v][:] if isinstance(v, str) and v in SCRATCH else v
@@ -79,105 +85,105 @@ def build(T, topo, core):
         op(name + "q", "V", ("g", b - a),
            lambda e, q: q.tensor_copy(B(dst + "q", a, b).bitcast(dt.uint32),
                                       B(src + "q", w0, w1).bitcast(dt.uint32).indirect(B(lst, l0, l1))),
-           [(src + "q", w0, w1), (lst, l0, l1)], [(dst + "q", a, b)], arr=arr)
+           [(src + "q", w0, w1), (lst, l0, l1)], [(dst + "q", a, b)], arr=[x + "q" for x in arr])
         op(name + "s", "VS", ("g", b - a),
            moved(lambda: B(dst + "s", a, b), lambda: B(src + "s", w0, w1).indirect(B(lst, l0, l1))),
-           [(src + "s", w0, w1), (lst, l0, l1)], [(dst + "s", a, b)], arr=arr)
+           [(src + "s", w0, w1), (lst, l0, l1)], [(dst + "s", a, b)], arr=[x + "s" for x in arr])
 
-    def mm(name, bank, st, s0, mv, a, b, start, stop, grp=None):
+    def mm(name, bank, st, s0, mv, a, b, start, stop, grp=None, arr=()):
         op(name, "P", ("p", b - a),
            lambda e, q: q.matmul_mx(B("ps", 512 * bank, 512 * bank + b - a), B(st + "q", s0, s0 + 128),
                                     B(st + "s", s0, s0 + 128), B(mv + "q", a, b), B(mv + "s", a, b), start, stop),
            [(st + "q", s0, s0 + 128), (st + "s", s0, s0 + 128), (mv + "q", a, b), (mv + "s", a, b)],
-           [("ps", bank, bank + 1)], grp=grp)
+           [("ps", bank, bank + 1)], grp=grp, arr=arr)
 
-    def vec(name, fn, R, W, n=1, f=1.0):
-        op(name, "V", ("e", n * f), fn, R, W)
-
-    def fill(buf, eng, after):
-        for h in range(4):
-            a, b = 240 * h, 240 * h + 240
-            op("fill%s%d" % (buf, h), eng, ("fill", 240),
-               lambda e, q, a=a, b=b: q.memset(B(buf, a, b), 0) if e == "V"
-               else q.iota(B(buf, a, b), [[0, 240]], 0, 0, allow_small_or_imprecise_dtypes=buf == "wb"), [], [(buf, a, b)], after=after)
-
-    kids = [("wa", 0), ("wb", 0), ("wb", 1)]
+    def vec(name, fn, R, W, n=1):
+        op(name, "V", ("e", n), fn, R, W)
 
     def rows(t, after, arr):
-        buf, r = kids[t]
-        return [dma("rows%d" % t, "Y", lambda: (T[buf][r:128:16, :], T["nxd%d" % t][:] if t else T.nx[:]), 30720, 16,
-                    [], [(buf, 0, 2 * NP, r)], after, arr)]
+        return [dma("rows%d" % t, "Y", lambda: (T.wb[t:128:16, :], T["nxd%d" % t][:] if t else T.nxb[:]), 15360, 16 if t else 128,
+                    [] if t else [("nxb", 0, 60)], [("wb", 0, 2 * NP, t)], after, arr)]
 
-    l = dma("ldst", "Y", lambda: (T.sti[:], T.st[:]), 12288, 128, [], [("sti", 0, 24)])
-    dma("ldnx", "S", lambda: (T.nxi[:], T.nx[:]), 30720, 128, [], [("nxi", 0, 60)], [l])
-    loads = {"ldk": ("kt", "k", 0, 4 * NP), "ldu": ("ut", "u", 0, 512),
+    dma("ldnx", "S", lambda: (T.nxi[:], T.nx[:]), 30720, 128, [], [("nxi", 0, 60)])
+    loads = {"ldst": ("sti", "st", 0, 24), "ldk": ("kt", "k", 0, 4 * NP), "ldu": ("ut", "u", 0, 512),
              "ldx0": ("xt", "x", 0, 4 * CUT), "ldx1": ("xt", "x", 4 * CUT, 4 * NT)}
     l = ["ldnx"]
     for name in LOADS:
         if name in loads:
             d, s, a, b = loads[name]
-            l = [dma(name, "Y", lambda d=d, s=s, a=a, b=b: (B(d, a, b), B(s, a, b)), 256 * (b - a), 128, [], [(d, a, b)], l)]
+            l = [dma(name, "Y", lambda d=d, s=s, a=a, b=b: (B(d, a, b), B(s, a, b)), (512 if d == "sti" else 256) * (b - a), 128,
+                     [], [(d, a, b)], l)]
         elif name == "ldw":
             l = [dma(name, "Y", lambda: (u8("wwq", 0, 512), T.wc[:]), 262144, 128, [], [("wwq", 0, 512)], l)]
         else:
             l = [dma(name, "Y", lambda: (T.wws[:], T.ws[:]), 65536, 128, [], [("wws", 0, 512)], l)]
 
-    for name, pat, cm, n, prev in [("jd", [[1, 128]], -1, 128, []), ("pi", [[0, 1]], 1, 1, ["iojd"]), ("lui", [[2, 8]], 0, 8, ["iopi"]),
-                                   ("j16", [[0, NM // 16], [1, 16]], 0, NM, ["iolui"])]:
+    for name, pat, cm, n in [("jd", [[1, 128]], -1, 128), ("pi", [[0, 1]], 1, 1), ("jr", [[0, NM], [1, 16]], 0, NM * 16)]:
         op("io" + name, "G", ("io", n),
            lambda e, q, name=name, pat=pat, cm=cm: q.iota(T[name][:], pat, 0, cm, allow_small_or_imprecise_dtypes=name[0] == "j"),
-           [], [(name, 0, n)], after=prev)
-    fill("wa", "VG", ["ioj16"])
+           [], [(name, 0, n)])
+    vec("zero", lambda e, q: q.memset(T.za[:], 0.0), [], [("za", 0, 516)], 258)
+    vec("za", lambda e, q: q.tensor_scalar(B("za", 3, 515, 4), T.jd[:], 0.0, None, EQ), [("jd", 0, 128)], [("za", 0, 516)], 64)
     for h in range(2):
-        vec("zero%d" % h, lambda e, q, h=h: q.memset(B("et", 1024 * h, 1024 * h + 1024), 0.0), [],
-            [("et", 1024 * h, 1024 * h + 1024)], 1024, 0.5)
+        a, b = NP * h, NP * h + NP
+        op("fill%d" % h, "VS", ("e", NP // 2, NP), affine(lambda a=a, b=b: B("wb", a, b), lambda: B("za", 0, NP), 0.0),
+           [("za", 0, NP)], [("wb", a, b)])
     for name, src, n, args in [
-            ("ident", "jd", 128, (0.0, None, EQ)), ("pa", "pi", 1, (4, 1, AluOpType.logical_shift_right, AluOpType.bitwise_and)),
+            ("pa", "pi", 1, (4, 1, AluOpType.logical_shift_right, AluOpType.bitwise_and)),
             ("pb", "pi", 1, (15, None, AluOpType.bitwise_and)), ("me", "pa", 1, (0.0, None, EQ)), ("mo", "pa", 1, (1.0, None, EQ)),
-            ("nxb", "nxi", 60, (-MID, None, ADD)), ("e15", "pb", 1, (15.0, None, EQ)), ("rs", "e15", 1, (31.0 / 64, 1.0 / 64, MUL, ADD)),
-            ("iv", "e15", 1, (-124.0, 128.0, MUL, ADD)), ("bi", "iv", 1, (MID, None, MUL)), ("me2", "pa", 1, (0.0, "iv", EQ, MUL)),
-            ("mo2", "pa", 1, (1.0, "iv", EQ, MUL)), ("pm1", "pb", 1, (1.0, None, ADD)), ("pm", "pb", 1, (1.0, None, MUL)),
-            ("lc", "pb", 1, (8.0, None, MUL)), ("lu", "lui", 8, (1.0, None, MUL)), ("off", "j16", NM, ("pm", None, AluOpType.not_equal)),
-            ("nxt", "j16", NM, ("pm1", 31.0, EQ, MUL)), ("p0", "sti", 24, ("iv", None, MUL))]:
-        vec(name, lambda e, q, name=name, src=src, n=n, args=args: q.tensor_scalar(B(name, 0, n), B(src, 0, n), *[val(v) for v in args]),
-            [(src, 0, n)] + [(v, 0, 1) for v in args if isinstance(v, str) and v in SCRATCH], [(name, 0, n)], n, 0.5)
-    vec("wt", lambda e, q: q.tensor_tensor(T.wt[:], T.off[:], T.nxt[:], ADD), [("off", 0, NM), ("nxt", 0, NM)], [("wt", 0, NM)], NM, 2)
-    for name, mask in [("ea", None), ("ee", "me"), ("eo", "mo")]:
-        for h in range(2):
-            for b in (2 * h, 2 * h + 1):
-                out, src = (lambda b=b: B("et", 513 * b, 512 * b + 512, 4)), (lambda: T.ident[:])
-                op("d%s%d" % (name, b), "VS", ("e", 128), affine(out, src, mask) if mask else moved(out, src),
-                   [("ident", 0, 128)] + ([(mask, 0, 1)] if mask else []), [("et", 512 * b, 512 * b + 512)])
-            quant("q%s%d" % (name, h), name, 256 * h, 256 * h + 256, "et", 1024 * h)
-    l = rows(0, l, [])
+            ("pm1", "pb", 1, (-1.0, None, ADD)), ("pm", "pb", 1, (1.0, None, MUL)),
+            ("nxb", "nxi", 60, (0.25, -MID / 4, MUL, ADD)),
+            ("off", "jr", NM * 8, ("pm1", None, AluOpType.not_equal)),
+            ("nxt", "jr", NM * 8, ("pm", 127.0, EQ, MUL))]:
+        vec(name, lambda e, q, name=name, src=src, args=args: q.tensor_scalar(T[name][:], T[src][:], *[val(v) for v in args]),
+            [(src, 0, 9999)] + [(v, 0, 1) for v in args if isinstance(v, str) and v in SCRATCH], [(name, 0, 9999)], n)
+    for name, src, s, c in [("dc", "me", 250.0, 500.0), ("c0", "me", 1000.0, -MID / 4), ("cl", "me", -8000.0, 2 * MID + 0.74)]:
+        op(name, "VS", ("e", 1), affine(lambda name=name: T[name][:], lambda src=src: T[src][:], s, c),
+           [(src, 0, 99)], [(name, 0, 99)])
+    op("dd", "VS", ("e", 1), affine(lambda: T.dd[:], lambda: B("jr", 0, 16 * NM, 8), "dc", -5000.0), [("jr", 0, 1), ("dc", 0, 1)], [("dd", 0, 99)])
+    vec("lu", lambda e, q: q.tensor_scalar(T.lu[:], B("jr", 0, 8), 16.0, None, MUL), [("jr", 0, 1)], [("lu", 0, 8)])
+    vec("wt", lambda e, q: q.tensor_tensor(T.wt[:], T.off[:], T.nxt[:], ADD), [("off", 0, 1), ("nxt", 0, 1)], [("wt", 0, 1)], 32 * NM)
+    vec("wt15", lambda e, q: q.tensor_scalar(B("wt", 15, 16 * NM, 16), B("wt", 15, 16 * NM, 16), 1.0 / 2048, None, MUL), [], [("wt", 0, 1)])
+    vec("p0", lambda e, q: q.tensor_scalar(B("pn0", 1, 48, 2), T.sti[:], 0.25, T.c0[:], MUL, ADD), [("sti", 0, 24), ("c0", 0, 1)], [("pn0", 0, 48)])
+    for name, mask in [("a", None), ("e", "me"), ("o", "mo")]:
+        if mask:
+            op("z" + name, "VS", ("e", 258, 516), affine(lambda name=name: T["z" + name][:], lambda: T.za[:], mask),
+               [("za", 0, 516), (mask, 0, 1)], [("z" + name, 0, 516)])
+        for b in range(4):
+            quant("qe%s%d" % (name, b), "e" + name, 128 * b, 128 * b + 128, "z" + name, 3 - b)
 
-    def send_nx(t, after):
+    def send(name, kind, a, b, after):
         def fn(e, q):
-            rid, pid = topo.addr(peer(t))[:2]
-            return q.remote_dma(T["nxd%d" % t][:], T.nxb[:], T.sem["anx%d" % t], T.sem.sent, pid, rid, topo.mask(core, peer(t)))
-        op("sn%d" % t, "G", ("rem", 15360, 128), fn, [("nxb", 0, 60)], [], "rem", after)
-    send_nx(1, ["ioj16"])
+            core, h = T.cores[rank], helper(T, topo, rank)
+            out = topo.mask(core, peer(1))
+            ways = []
+            for to, mask, nx, tb, sem in [(peer(1), out, "nxd1", "tb1", "a1"), (h, topo.mask(core, h) & ~out, "nxh", "tbh", "ah")]:
+                rid, pid = topo.addr(to)[:2]
+                view = u8 if kind == "q" else B
+                src, dst = (T.nxb[:], T[nx][:]) if kind == "n" else (view("tb0" + kind, a, b), view(tb + kind, a, b))
+                ways.append(RemoteDMATransfer(dst_ids=[DstId(rid=rid, pnc=pid)], dma_engine_mask=mask, remote_sem=T.sem[sem + name],
+                                              src=src, dst=dst))
+            return q.remote_dma_fused(ways, local_sem=T.sem.sent)
+        nbytes = {"n": 256, "q": 512, "s": 128}[kind] * (b - a)
+        op("s" + name, "G", ("rem", nbytes, 128), fn, [("nxb" if kind == "n" else "tb0" + kind, a, b)], [], "rem", after)
 
-    def send(name, t, kind, a, b, after, arr=()):
-        def fn(e, q):
-            rid, pid = topo.addr(peer(t))[:2]
+        def on_fn(e, q):
+            h = helper(T, topo, rank)
+            rid, pid = topo.addr(peer(2))[:2]
             view = u8 if kind == "q" else B
-            return q.remote_dma(view("tb%d%s" % (t, kind), a, b), view("tb0" + kind, a, b), T.sem["atb%d" % t], T.sem.sent,
-                                pid, rid, topo.mask(core, peer(t)))
-        op(name, "G", ("rem", (512 if kind == "q" else 128) * (b - a), 128), fn, [("tb0" + kind, a, b)], [], "rem", after, arr)
+            src, dst = (T.nxh[:], T.nxd2[:]) if kind == "n" else (view("tbh" + kind, a, b), view("tb2" + kind, a, b))
+            return q.remote_dma(dst, src, T.sem["a2" + name], T.sem.sent, pid, rid, topo.mask(h, peer(2)))
+        op("h" + name, "H", ("rem", nbytes, 8 if kind == "n" else 128), on_fn, [], [], "rem",
+           ["h" + x[1:] for x in after if x[0] == "s"], ["ah" + name])
+        return ["s" + name]
 
+    s = send("n", "n", 0, 60, [])
+    l = rows(0, l, [])
     quant("qk", "tb0", 0, NP, "kt", 0)
     quant("qu", "uu", 0, 128, "ut", 0)
-    pick("pku", "tb0", NP, TW, "uu", 0, 128, "lc", 0)
-    send("s1b", 1, "q", 0, TW, ["sn1", "rows0"])
-    send("s1s", 1, "s", 0, TW, ["s1b"])
-    fill("wb", "G", ["s1s"])
-    l = rows(1, l, ["anx1"])
-    send("s2c", 2, "q", 0, TW, l, ["anx1"])
-    send("s2s", 2, "s", 0, TW, ["s2c"])
-    send_nx(2, ["s2s"])
-    dma("ldv", "Y", lambda: (T.vt[:], T.v[:]), 131072, 128, [], [("vt", 0, 512)], l, ["atb1"])
-    quant("qv", "vv", 0, 128, "vt", 0)
+    pick("su", "tb0", NP, TW, "uu", 0, 128, "lu", 0)
+    for name, kind, a, b in [("tq", "q", 0, NP), ("ts", "s", 0, NP), ("uq", "q", NP, TW), ("us", "s", NP, TW)]:
+        s = send(name, kind, a, b, s)
     for t in range(4):
         vec("l0%d" % t, lambda e, q, t=t: q.tensor_scalar(B("l0", 24 * t, 24 * t + 24), T.sti[:], 4.0, float(t), MUL, ADD),
             [("sti", 0, 24)], [("l0", 24 * t, 24 * t + 24)])
@@ -185,7 +191,7 @@ def build(T, topo, core):
     def hop(t, c):
         a, b = CH[c]
         n, la, lb, k0 = b - a, a // 16, b // 16, 4 * c
-        tag, arr = "%d%d" % (t, c), (["atb%d" % t] if t else [])
+        m, tag = lb - la, "%d%d" % (t, c)
         z, zn, bl, bt, rt = "z%d" % t, "z%d" % (t + 1), "bl%d" % t, "bt%d" % t, "rt%d" % t
 
         def bank(i):
@@ -199,7 +205,8 @@ def build(T, topo, core):
             quant("qx%d" % c, "z0", a, b, "xt", 4 * a)
             terms = [("ea", "ng", a), ("ea", "z0", a)]
         else:
-            pick("pe" + tag, "pk%d" % t, 2 * a, 2 * b, "tb%d" % t, 0, NP, "lp%d" % t, 2 * la, arr)
+            for h, x0 in enumerate((2 * a, a + b)):
+                pick("pe%s%d" % (tag, h), "pk%d" % t, x0, x0 + n, "tb%d" % t, 0, NP, "lp%d" % t, x0 // 16, ["a%dt" % t])
             terms = [("ea", z, a), ("ee", "pk%d" % t, 2 * a), ("eo", "pk%d" % t, a + b)]
         for j, (st, mv, m0) in enumerate(terms):
             for i in range(4):
@@ -208,37 +215,35 @@ def build(T, topo, core):
             op("eb%s%d" % (tag, i), "VS", ("e", n), affine(lambda i=i: B(bt, 4 * a + i, 4 * b, 4), lambda i=i: bank(i), 0.5),
                [], [("ps", k0 + i, k0 + i + 1), (bt, 4 * a, 4 * b, i)])
         quant("qb" + tag, bl, a, b, bt, 4 * a)
-        mm("ms" + tag, k0, "su%d" % t, 0, bl, a, b, True, True)
-        bit, sa, lf, ln, pn, (win, row) = "bit%d" % t, "sa%d" % t, "lf%d" % t, "ln%d" % t, "p%d" % t, kids[t]
+        mm("ms" + tag, k0, "tb%d" % t, NP, bl, a, b, True, True, arr=["a%duq" % t, "a%dus" % t] if t else [])
+        bit, sa, lf, ln, pn = ["%s%d" % (s, t) for s in ("bit", "sa", "lf", "ln", "pn")]
         op("gt" + tag, "S", ("e", n), lambda e, q: q.activation(B(bit, a, b), bank(0), ActivationFunctionType.Sign, bias=-2.0 ** -120),
            [], [("ps", k0, k0 + 1), (bit, a, b)])
-        vec("sa" + tag, lambda e, q: q.tensor_tensor_scan(B(sa, a, b), B("wt", 0, n), B(bit, a, b), 0.0, MUL, ADD),
-            [("wt", 0, n), (bit, a, b)], [(sa, a, b)], n, 0.5)
+        vec("sa" + tag, lambda e, q: q.tensor_tensor_scan(B(sa, a, b), B(bit, a, b), B("wt", 0, n), 0.0, ADD, MUL),
+            [("wt", 0, 1), (bit, a, b)], [(sa, a, b)], n // 2)
         rep = 2 if t < NH - 1 else 1
-        f0, f1 = 2 * la, 2 * la + rep * (lb - la)
+        f0, f1 = 2 * la, 2 * la + rep * m
         for r in range(rep):
-            vec("lf%s%d" % (tag, r), lambda e, q, r=r: q.tensor_tensor(B(lf, f0 + r, f1, rep), B(sa, a + 15, b, 16), B(pn, la, lb), ADD),
-                [(sa, a, b), (pn, la, lb)], [(lf, f0, f1, r)])
-        vec("ln" + tag, lambda e, q: q.tensor_scalar(B(ln, f0, f1), B(lf, f0, f1), T.rs[:], 0.74, MUL, ADD),
-            [(lf, f0, f1), ("rs", 0, 1)], [(ln, f0, f1)])
+            vec("lf%s%d" % (tag, r), lambda e, q, r=r: q.tensor_tensor(B(lf, f0 + r, f1, rep), B(sa, a + 15, b, 16), B(pn, 2 * la + 1, 2 * lb, 2), ADD),
+                [(sa, a, b), (pn, 2 * la, 2 * lb)], [(lf, f0, f1, r)])
+        vec("ln" + tag, lambda e, q: q.tensor_scalar(B(ln, f0, f1), B(lf, f0, f1), 8.0, T.cl[:], MUL, ADD),
+            [(lf, f0, f1), ("cl", 0, 1)], [(ln, f0, f1)])
         if t == NH - 1:
-            op("pl" + tag, "VS", ("g", n), affine(lambda: B("plb", a, b), lambda: T[win][:].indirect(B(ln, f0, f1)), 1.0, MID),
-               [(win, 0, 2 * NP), (ln, f0, f1)], [("plb", a, b)])
+            op("pl" + tag, "VS", ("g", n), affine(lambda: B("plb", a, b), lambda: T.wb[:].indirect(B(ln, f0, f1)), 4.0, MID),
+               [("wb", 0, 2 * NP), (ln, f0, f1)], [("plb", a, b)])
         else:
-            gm, sb, xa, lp, p2 = ["%s%d" % (s, t + 1) for s in ("gm", "sb", "xa", "lp", "p")]
-            op("gm" + tag, "VS" if t else "V", ("g", 2 * n),
-               affine(lambda: B(gm, 2 * a, 2 * b), lambda: T[win][:].indirect(B(ln, f0, f1)), 1.0, None if t else -MID),
-               [(win, 0, 2 * NP), (ln, f0, f1)], [(gm, 2 * a, 2 * b)])
-            vec("sb" + tag, lambda e, q: q.transpose(B(sb, 2 * a, 2 * b), B(gm, 2 * a, 2 * b)),
-                [(gm, 2 * a, 2 * b)], [(sb, 2 * a, 2 * b)], 2 * n, 0.5)
-            for h, m in enumerate(("me2", "mo2")):
-                x0, x1, src = 2 * la + h * (lb - la), la + lb + h * (lb - la), (lambda h=h: B(sb, 2 * a + 16 * h + row, 2 * b, 32))
-                vec("lp%s%d" % (tag, h), lambda e, q, x0=x0, x1=x1, src=src: q.tensor_scalar(B(lp, x0, x1), src(), MID, None, ADD),
-                    [(sb, 2 * a, 2 * b)], [(lp, x0, x1)])
-                op("ph%s%d" % (tag, h), "VS", ("e", 1), affine(lambda x0=x0, x1=x1: B(xa, x0, x1), src, m, None if h else "bi"),
-                   [(sb, 2 * a, 2 * b), (m, 0, 1), ("bi", 0, 1)], [(xa, x0, x1)])
-            vec("p2" + tag, lambda e, q: q.tensor_tensor(B(p2, la, lb), B(xa, 2 * la, la + lb), B(xa, la + lb, 2 * lb), ADD),
-                [(xa, 2 * la, 2 * lb)], [(p2, la, lb)])
+            gm, sb, lp, nb = ["%s%d" % (s, t + 1) for s in ("gm", "sb", "lp", "pn")]
+            op("gm" + tag, "VS", ("g", 2 * n), moved(lambda: B(gm, 2 * a, 2 * b), lambda: T.wb[:].indirect(B(ln, f0, f1))),
+               [("wb", 0, 2 * NP), (ln, f0, f1)], [(gm, 2 * a, 2 * b)])
+            vec("sb" + tag, lambda e, q: q.transpose(B(sb, 2 * a, 2 * b), B(gm, 2 * a, 2 * b)), [(gm, 2 * a, 2 * b)], [(sb, 2 * a, 2 * b)], n)
+            for h in range(2):
+                x0 = 2 * la + h * m
+                vec("lp%s%d" % (tag, h),
+                    lambda e, q, x0=x0, h=h: q.tensor_scalar(B(lp, x0, x0 + m), B(sb, 2 * a + 16 * h + t, 2 * b, 32), 4.0, MID, MUL, ADD),
+                    [(sb, 2 * a, 2 * b)], [(lp, x0, x0 + m)])
+            vec("ph" + tag, lambda e, q: q.tensor_tensor_scan(B(nb, 2 * la, 2 * lb), B("dd", 0, 2 * m), B(sb, 2 * a + t, 2 * b, 16), 0.0,
+                                                              ADD, AluOpType.max),
+                [(sb, 2 * a, 2 * b), ("dd", 0, 1)], [(nb, 2 * la, 2 * lb)])
         for i in (1, 2, 3, 0):
             mm("mr%s%d" % (tag, i), k0 + i, "ww", 128 * i, bl, a, b, True, True)
             op("er%s%d" % (tag, i), "VS", ("e", n), affine(lambda i=i: B(rt, 4 * a + i, 4 * b, 4), lambda i=i: bank(i), 0.03125),
@@ -251,20 +256,21 @@ def build(T, topo, core):
             dma("stc%d" % c, "YS", lambda: (B("oc", 4 * a, 4 * b), u8(zn + "q", a, b)), 512 * n, 128, [(zn + "q", a, b)], [])
 
     for t in range(NH):
-        pick("su%d" % t, "su%d" % t, 0, 128, "tb%d" % t, NP, TW, "lu", 0, ["atb%d" % t] if t else [])
-        if t == 2:
-            rows(2, ["ldv"], ["anx2"])
         for c in range(2):
-            cur[0] = c
             hop(t, c)
-            cur[0] = None
+        if t < NH - 1:
+            l = rows(t + 1, l, ["a%dn" % (t + 1)])
+        if t == 0:
+            l = [dma("ldv", "Y", lambda: (T.vt[:], T.v[:]), 131072, 128, [], [("vt", 0, 512)], l)]
+            quant("qv", "vv", 0, 128, "vt", 0)
     for k in range(4):
         dma("sts%d" % k, "YS", lambda k=k: (T.osc[4 * k:4 * k + 4, :], T.z3s[32 * k:32 * k + 4, :]), 1536, 4, [("z3s", 0, NT)], [])
-    dma("stp", "YS", lambda: (T.pl[:], T.plb[kids[2][1]:128:16, :]), 12288, 16, [("plb", 0, NT)], [])
+    dma("stp", "YS", lambda: (T.pl[:], T.plb[NH - 1:128:16, :]), 12288, 16, [("plb", 0, NT)], [])
     return ops
 
 
-ARR = {"anx1": (["sn1"], 1, 1), "anx2": (["sn2"], 2, 1), "atb1": (["s1b", "s1s"], 1, 2), "atb2": (["s2c", "s2s"], 2, 2)}
+PIECES = ["n", "tq", "ts", "uq", "us"]
+ARR = {w + p: ("h" if w == "a2" else "s") + p for w in ("a1", "a2", "ah") for p in PIECES}
 
 
 def overlap(r, s):
@@ -281,7 +287,7 @@ def link(ops):
 
 
 ORDER = """
-16V 0Y 1S 8G 2Y 3Y 4Y 5Y 9G 6Y 7Y 10G 18V 19V 11G 38S 20V 17V 39S 14G 40V 41S 42S 24V 21V 33V 13G 45S 26V 44S 75V 77V 43V 15G 30V 47S 46V 48S 23V 76V 12G 22V 49V 51S 74V 57G 56Y 58V 82S 80S 32V 59V 83S 81V 122S 60V 31V 61V 84V 121S 62G 85V 87P 88P 124S 123V 92P 63G 86P 27V 96S 90P 35V 91P 78V 66G 94S 89P 93P 95S 25V 125V 97S 36V 64G 127P 34V 79S 129P 128P 50S 65G 126V 98V 133P 37V 137S 99P 67G 131P 100S 132P 52V 130P 54S 134P 136S 101V 116P 68Y 69G 53V 114P 135S 112P 102V 103V 138S 118P 70G 55V 117S 104V 139V 115S 71G 119S 105V 140P 157P 141S 153P 154S 159P 142V 155P 106V 113S 144V 156S 143V 107V 160S 109V 145V 120V 158S 146V 169P 166P 167P 168P 161V 147V 207P 208P 209P 164V 163S 72Y 210P 165S 148V 150V 28V 205V 206S 173P 172P 176P 170P 174P 29V 180S 177P 171P 178S 175P 181S 214P 179V 218P 211P 162V 222S 213P 215P 110V 151S 108V 217P 182V 212P 221S 216P 183P 219S 220V 198P 200P 184S 111V 223V 196P 199S 185V 224P 149S 201V 197S 202P 186V 239P 225S 187V 241P 152V 188V 203S 243P 226V 237P 189S 227V 228V 204V 229V 251P 230S 252P 190V 254P 253P 191V 193V 238V 250S 248Y 249V 244S 231V 256P 242S 258P 240V 233S 255P 192S 232V 260P 235S 234V 259P 245V 288S 262P 287V 257P 291P 261P 290P 194S 292P 263S 264V 289P 296P 265S 246V 300P 266S 294P 73V 298P 247S 295P 267V 299P 302S 293P 195V 304V 297P 303S 268P 301V 278P 269S 276P 236V 274P 305V 277S 280P 279V 275S 306P 316P 281V 307S 314P 270V 312P 315S 282V 318P 313S 317V 286Y 283P 319V 284S 308V 320V 285S 309V 326Y 321P 271V 324Y 310V 328Y 272V 325Y 311S 322V 327Y 273V 323Y 329Y
+0S 9G 8G 11V 15V 16V 17V 18V 12V 20V 19V 10G 35V 13V 23V 34V 26S 24S 36S 14S 41S 27S 1Y 2Y 3Y 4Y 5Y 6Y 7Y 62V 32V 21V 64V 48Y 28V 61V 37V 63V 33V 107V 104V 105S 106S 65S 66S 68S 67S 49V 108V 70V 109V 44V 42V 69V 25S 111P 113P 110P 112P 116P 117P 114P 115P 120S 121S 119S 118S 74P 73P 71P 78P 77P 72P 76P 75P 50V 22V 51V 29V 122V 31V 30V 39V 80V 40V 52S 82S 81S 79S 83V 123P 138P 134P 136P 124S 140P 135S 137S 141S 84P 85S 95P 97P 101P 99P 46G 53G 55G 57G 59G 47H 54H 56H 58H 60H 125V 139V 127V 126V 45V 128V 38V 86V 142V 88V 87V 96S 192P 191P 193P 194P 98S 129S 102S 100V 89V 130V 90S 103V 131V 132V 187V 152P 151P 150P 153P 188S 190S 91V 189V 92V 93V 43V 146V 147S 196P 197P 198P 195P 202P 201P 199P 200P 149S 206S 204S 148V 154P 155P 156P 159P 157P 161P 160P 158P 163S 165S 164S 203V 205V 133V 207V 94V 162V 166V 143Y 208P 223P 221P 219P 209S 225P 224S 220S 226S 167P 168S 178P 182P 180P 184P 210V 222V 212V 211V 213V 179S 214S 181S 227V 169V 183V 171V 170V 185V 172V 173S 144Y 228Y 215V 186V 216V 217V 269V 273P 274P 276P 275P 270S 272S 174V 271V 234P 236P 235P 233P 175V 230S 177V 176V 229V 280P 277P 278P 279P 283P 282P 281P 284P 232S 286S 288S 231V 239P 240P 238P 243P 244P 237P 241P 242P 247S 287V 285V 218V 289V 145V 290P 248S 245S 246V 249V 291S 300P 296P 298P 301V 302P 297S 299S 303V 292V 304V 250P 258P 260P 256P 251S 261S 259S 262P 257V 263V 252V 264V 253V 293V 254V 294V 305P 265P 308Y 306S 307S 266V 309Y 255V 311S 312S 268Y 310Y 267Y 295S 313S
 """
 _OPS = build(None, None, None)
 PLAN = [(int(w[:-1]), w[-1]) for w in ORDER.split()]
@@ -289,15 +295,31 @@ SEMAPHORES = ["cV", "cS", "cP", "cG", "sent"] + sorted(ARR) + ["d" + o["name"] f
 
 
 def rank_program(g, core, T, topo):
-    rank, n = T.rank_of(core), len(T.cores)
-    if rank is None:
+    n = len(T.cores)
+    rank = T.rank_of(core)
+    served = [r for r in range(n) if helper(T, topo, r) == core]
+    if rank is None and not served:
         return
-    ops = link(build(T, topo, core))
-    arrive = {a: ARR[a][2] * len(topo.engines(T.cores[(rank + ARR[a][1]) % n], core)) for a in ARR}
+    if served:
+        rank = served[0]
+        src, to = T.cores[rank], T.cores[(rank - 2) % n]
+        came = len(topo.engines(src, core)) - len(topo.engines(src, T.cores[(rank - 1) % n]))
+        ops = build(T, topo, rank)
+        steps = [ops[i] for i, e in PLAN if e == "H"]
+        for o in steps:
+            g.wait_ge(T.sem[o["arr"][0]], came)
+            o["fn"]("H", g)
+        g.wait_ge(T.sem.sent, len(steps) * len(topo.engines(core, to)))
+        return
+    ops = link(build(T, topo, rank))
+    far = {"a1": T.cores[(rank + 1) % n], "a2": helper(T, topo, (rank + 2) % n)}
+    arrive = {a: len(topo.engines(far[a[:2]], core)) for a in ARR if a[:2] in far}
     queue = {"V": g.vector, "S": g.scalar, "P": g.tensor, "G": g, "Y": g.sync}
     known = {e: {} for e in queue}
     count, event = dict(arrive), {}
     for i, e in PLAN:
+        if e == "H":
+            continue
         o, q, kn = ops[i], queue[e], known[e]
         top = {}
         for s, v, clock in [event[j] for j in o["dep"]] + [(a, arrive[a], {}) for a in o["arr"]]:
@@ -312,11 +334,12 @@ def rank_program(g, core, T, topo):
                     kn[s2] = max(kn.get(s2, 0), v2)
         ins = o["fn"](e, q)
         if o["kind"] == "rem":
-            s, inc = "sent", len(topo.engines(core, T.cores[(rank - int(o["name"].replace("n", "")[1])) % n]))
+            s, inc = "sent", len(topo.engines(core, helper(T, topo, rank)))
         else:
             s, inc = ("c" + e, 1) if o["kind"] == "c" else ("d" + o["name"], 16)
             ins.then_inc(T.sem[s], inc)
         count[s] = count.get(s, 0) + inc
         event[i] = (s, count[s], dict(kn))
-    for s in sorted(count):
+    last = {s: k for k, (s, v, clock) in enumerate([event[i] for i, e in PLAN if e != "H"])}
+    for s in sorted(count, key=lambda s: last.get(s, -1)):
         g.wait_ge(T.sem[s], count[s])

from concourse.bass import DstId, RemoteDMATransfer
from concourse.mybir import dt, AluOpType, ActivationFunctionType

NT, NP, NH = 384, 480, 3
CUT = 192
TW = NP + 128
MID = 240.0
LOADS = ["ldst", "ldk", "ldx0", "ldx1", "ldu", "ldw", "ldws"]
CH = [(0, CUT), (CUT, NT)]
NM = max(CUT, NT - CUT) // 16
X4, U8, BF, F32, I32, U16 = "float8_e4m3fn_x4", "uint8", "bfloat16", "float32", "int32", "uint16"

SCRATCH = {"ps": ("psum", [128, 4096], F32), "nxh": ("dram", [128, 60], BF)}
_S = [("kt", 4 * NP, BF), ("xt", 4 * NT, BF), ("ut", 512, BF), ("vt", 512, BF), ("sti", 24, I32),
      ("jd", 128, BF), ("za", 516, BF), ("ze", 516, BF), ("zo", 516, BF), ("pi", 1, I32), ("pa", 1, I32), ("pb", 1, I32),
      ("wb", 2 * NP, BF), ("nxi", 60, I32), ("nxb", 60, BF), ("lu", 8, U16), ("l0", 96, U16),
      ("kg", 4 * NT, BF), ("yb", NT, F32), ("plb", NT, F32), ("dd", 2 * NM, F32)]
_S += [(_n, 1, F32) for _n in ("pm", "pm1", "me", "mo", "dc", "c0", "cl")]
_S += [(_n, 16 * NM, BF) for _n in ("jr", "off", "nxt", "wt")]
_M = [("uu", 128), ("vv", 128), ("ww", 512), ("ea", 512), ("ee", 512), ("eo", 512), ("ng", NT), ("z0", NT), ("tbh", TW)]
for _t in range(NH):
    _M += [("tb%d" % _t, TW), ("bl%d" % _t, NT), ("z%d" % (_t + 1), NT)]
    _S += [("bt%d" % _t, 4 * NT, BF), ("rt%d" % _t, 4 * NT, BF), ("ln%d" % _t, 48, U16),
           ("bit%d" % _t, NT, BF), ("sa%d" % _t, NT, BF), ("lf%d" % _t, 48, F32), ("pn%d" % _t, 48, F32)]
    if _t > 0:
        SCRATCH["nxd%d" % _t] = ("dram", [128, 60], BF)
        _M += [("pk%d" % _t, 2 * NT)]
        _S += [("gm%d" % _t, 2 * NT, BF), ("sb%d" % _t, 2 * NT, BF), ("lp%d" % _t, 48, U16)]
for _n, _c in _M:
    _S += [(_n + "q", _c, X4), (_n + "s", _c, U8)]
for _n, _c, _d in _S:
    SCRATCH[_n] = ("sbuf", [128, _c], _d)

ADD, MUL, EQ = AluOpType.add, AluOpType.mult, AluOpType.is_equal
COPY, IDENT = ActivationFunctionType.Copy, ActivationFunctionType.Identity


def helper(T, topo, rank):
    core, to = T.cores[rank], T.cores[(rank - 2) % len(T.cores)]
    return [c for c in topo.cores_of(core) if topo.die(c) != topo.die(core) and T.rank_of(c) is None and topo.may_write(c, to)][0]


def build(T, topo, rank):
    ops = []

    def op(name, eng, cost, fn, R=(), W=(), kind="c", after=(), arr=(), grp=None):
        ops.append({"name": name, "eng": eng, "cost": cost, "fn": fn, "R": list(R), "W": list(W), "kind": kind,
                    "after": list(after), "arr": list(arr), "grp": grp})
        return name

    def B(n, a, b, s=1):
        return T[n][:, a:b:s] if s != 1 else T[n][:, a:b]

    def u8(n, a, b):
        return T[n][:, a:b].bitcast(dt.uint8)

    def dma(name, eng, pair, nbytes, rows, R, W, after=(), arr=()):
        return op(name, eng, ("dma", nbytes, rows), lambda e, q: q.dma_start(*pair()), R, W, "dma", after, arr)

    def peer(t):
        return T.cores[(rank - t) % len(T.cores)]

    def val(v):
        return T[v][:] if isinstance(v, str) and v in SCRATCH else v

    def affine(out, src, s, c=None):
        def fn(e, q):
            if e == "V":
                return q.tensor_scalar(out(), src(), val(s), None, MUL) if c is None else q.tensor_scalar(out(), src(), val(s), val(c), MUL, ADD)
            if isinstance(s, str) or c is not None:
                return q.activation(out(), src(), IDENT, bias=0.0 if c is None else val(c), scale=val(s))
            return q.activation(out(), src(), COPY, scale=s)
        return fn

    def moved(out, src):
        return lambda e, q: q.tensor_copy(out(), src()) if e == "V" else q.activation(out(), src(), COPY)

    def quant(name, dst, a, b, src, s0):
        s1 = s0 + 4 * (b - a)
        op(name, "V", ("q", s1 - s0), lambda e, q: q.quantize_mx(B(dst + "q", a, b), B(dst + "s", a, b), B(src, s0, s1)),
           [(src, s0, s1)], [(dst + "q", a, b), (dst + "s", a, b)])

    def pick(name, dst, a, b, src, w0, w1, lst, l0, arr=()):
        l1 = l0 + (b - a) // 16
        op(name + "q", "V", ("g", b - a),
           lambda e, q: q.tensor_copy(B(dst + "q", a, b).bitcast(dt.uint32),
                                      B(src + "q", w0, w1).bitcast(dt.uint32).indirect(B(lst, l0, l1))),
           [(src + "q", w0, w1), (lst, l0, l1)], [(dst + "q", a, b)], arr=[x + "q" for x in arr])
        op(name + "s", "VS", ("g", b - a),
           moved(lambda: B(dst + "s", a, b), lambda: B(src + "s", w0, w1).indirect(B(lst, l0, l1))),
           [(src + "s", w0, w1), (lst, l0, l1)], [(dst + "s", a, b)], arr=[x + "s" for x in arr])

    def mm(name, bank, st, s0, mv, a, b, start, stop, grp=None, arr=()):
        op(name, "P", ("p", b - a),
           lambda e, q: q.matmul_mx(B("ps", 512 * bank, 512 * bank + b - a), B(st + "q", s0, s0 + 128),
                                    B(st + "s", s0, s0 + 128), B(mv + "q", a, b), B(mv + "s", a, b), start, stop),
           [(st + "q", s0, s0 + 128), (st + "s", s0, s0 + 128), (mv + "q", a, b), (mv + "s", a, b)],
           [("ps", bank, bank + 1)], grp=grp, arr=arr)

    def vec(name, fn, R, W, n=1):
        op(name, "V", ("e", n), fn, R, W)

    def rows(t, after, arr):
        return [dma("rows%d" % t, "Y", lambda: (T.wb[t:128:16, :], T["nxd%d" % t][:] if t else T.nxb[:]), 15360, 16 if t else 128,
                    [] if t else [("nxb", 0, 60)], [("wb", 0, 2 * NP, t)], after, arr)]

    dma("ldnx", "S", lambda: (T.nxi[:], T.nx[:]), 30720, 128, [], [("nxi", 0, 60)])
    loads = {"ldst": ("sti", "st", 0, 24), "ldk": ("kt", "k", 0, 4 * NP), "ldu": ("ut", "u", 0, 512),
             "ldx0": ("xt", "x", 0, 4 * CUT), "ldx1": ("xt", "x", 4 * CUT, 4 * NT)}
    l = ["ldnx"]
    for name in LOADS:
        if name in loads:
            d, s, a, b = loads[name]
            l = [dma(name, "Y", lambda d=d, s=s, a=a, b=b: (B(d, a, b), B(s, a, b)), (512 if d == "sti" else 256) * (b - a), 128,
                     [], [(d, a, b)], l)]
        elif name == "ldw":
            l = [dma(name, "Y", lambda: (u8("wwq", 0, 512), T.wc[:]), 262144, 128, [], [("wwq", 0, 512)], l)]
        else:
            l = [dma(name, "Y", lambda: (T.wws[:], T.ws[:]), 65536, 128, [], [("wws", 0, 512)], l)]

    for name, pat, cm, n in [("jd", [[1, 128]], -1, 128), ("pi", [[0, 1]], 1, 1), ("jr", [[0, NM], [1, 16]], 0, NM * 16)]:
        op("io" + name, "G", ("io", n),
           lambda e, q, name=name, pat=pat, cm=cm: q.iota(T[name][:], pat, 0, cm, allow_small_or_imprecise_dtypes=name[0] == "j"),
           [], [(name, 0, n)])
    vec("zero", lambda e, q: q.memset(T.za[:], 0.0), [], [("za", 0, 516)], 258)
    vec("za", lambda e, q: q.tensor_scalar(B("za", 3, 515, 4), T.jd[:], 0.0, None, EQ), [("jd", 0, 128)], [("za", 0, 516)], 64)
    for h in range(2):
        a, b = NP * h, NP * h + NP
        op("fill%d" % h, "VS", ("e", NP // 2, NP), affine(lambda a=a, b=b: B("wb", a, b), lambda: B("za", 0, NP), 0.0),
           [("za", 0, NP)], [("wb", a, b)])
    for name, src, n, args in [
            ("pa", "pi", 1, (4, 1, AluOpType.logical_shift_right, AluOpType.bitwise_and)),
            ("pb", "pi", 1, (15, None, AluOpType.bitwise_and)), ("me", "pa", 1, (0.0, None, EQ)), ("mo", "pa", 1, (1.0, None, EQ)),
            ("pm1", "pb", 1, (-1.0, None, ADD)), ("pm", "pb", 1, (1.0, None, MUL)),
            ("nxb", "nxi", 60, (0.25, -MID / 4, MUL, ADD)),
            ("off", "jr", NM * 8, ("pm1", None, AluOpType.not_equal)),
            ("nxt", "jr", NM * 8, ("pm", 127.0, EQ, MUL))]:
        vec(name, lambda e, q, name=name, src=src, args=args: q.tensor_scalar(T[name][:], T[src][:], *[val(v) for v in args]),
            [(src, 0, 9999)] + [(v, 0, 1) for v in args if isinstance(v, str) and v in SCRATCH], [(name, 0, 9999)], n)
    for name, src, s, c in [("dc", "me", 250.0, 500.0), ("c0", "me", 1000.0, -MID / 4), ("cl", "me", -8000.0, 2 * MID + 0.74)]:
        op(name, "VS", ("e", 1), affine(lambda name=name: T[name][:], lambda src=src: T[src][:], s, c),
           [(src, 0, 99)], [(name, 0, 99)])
    op("dd", "VS", ("e", 1), affine(lambda: T.dd[:], lambda: B("jr", 0, 16 * NM, 8), "dc", -5000.0), [("jr", 0, 1), ("dc", 0, 1)], [("dd", 0, 99)])
    vec("lu", lambda e, q: q.tensor_scalar(T.lu[:], B("jr", 0, 8), 16.0, None, MUL), [("jr", 0, 1)], [("lu", 0, 8)])
    vec("wt", lambda e, q: q.tensor_tensor(T.wt[:], T.off[:], T.nxt[:], ADD), [("off", 0, 1), ("nxt", 0, 1)], [("wt", 0, 1)], 32 * NM)
    vec("wt15", lambda e, q: q.tensor_scalar(B("wt", 15, 16 * NM, 16), B("wt", 15, 16 * NM, 16), 1.0 / 2048, None, MUL), [], [("wt", 0, 1)])
    vec("p0", lambda e, q: q.tensor_scalar(B("pn0", 1, 48, 2), T.sti[:], 0.25, T.c0[:], MUL, ADD), [("sti", 0, 24), ("c0", 0, 1)], [("pn0", 0, 48)])
    for name, mask in [("a", None), ("e", "me"), ("o", "mo")]:
        if mask:
            op("z" + name, "VS", ("e", 258, 516), affine(lambda name=name: T["z" + name][:], lambda: T.za[:], mask),
               [("za", 0, 516), (mask, 0, 1)], [("z" + name, 0, 516)])
        for b in range(4):
            quant("qe%s%d" % (name, b), "e" + name, 128 * b, 128 * b + 128, "z" + name, 3 - b)

    def send(name, kind, a, b, after):
        def fn(e, q):
            core, h = T.cores[rank], helper(T, topo, rank)
            out = topo.mask(core, peer(1))
            ways = []
            for to, mask, nx, tb, sem in [(peer(1), out, "nxd1", "tb1", "a1"), (h, topo.mask(core, h) & ~out, "nxh", "tbh", "ah")]:
                rid, pid = topo.addr(to)[:2]
                view = u8 if kind == "q" else B
                src, dst = (T.nxb[:], T[nx][:]) if kind == "n" else (view("tb0" + kind, a, b), view(tb + kind, a, b))
                ways.append(RemoteDMATransfer(dst_ids=[DstId(rid=rid, pnc=pid)], dma_engine_mask=mask, remote_sem=T.sem[sem + name],
                                              src=src, dst=dst))
            return q.remote_dma_fused(ways, local_sem=T.sem.sent)
        nbytes = {"n": 256, "q": 512, "s": 128}[kind] * (b - a)
        op("s" + name, "G", ("rem", nbytes, 128), fn, [("nxb" if kind == "n" else "tb0" + kind, a, b)], [], "rem", after)

        def on_fn(e, q):
            h = helper(T, topo, rank)
            rid, pid = topo.addr(peer(2))[:2]
            view = u8 if kind == "q" else B
            src, dst = (T.nxh[:], T.nxd2[:]) if kind == "n" else (view("tbh" + kind, a, b), view("tb2" + kind, a, b))
            return q.remote_dma(dst, src, T.sem["a2" + name], T.sem.sent, pid, rid, topo.mask(h, peer(2)))
        op("h" + name, "H", ("rem", nbytes, 8 if kind == "n" else 128), on_fn, [], [], "rem",
           ["h" + x[1:] for x in after if x[0] == "s"], ["ah" + name])
        return ["s" + name]

    s = send("n", "n", 0, 60, [])
    l = rows(0, l, [])
    quant("qk", "tb0", 0, NP, "kt", 0)
    quant("qu", "uu", 0, 128, "ut", 0)
    pick("su", "tb0", NP, TW, "uu", 0, 128, "lu", 0)
    for name, kind, a, b in [("tq", "q", 0, NP), ("ts", "s", 0, NP), ("uq", "q", NP, TW), ("us", "s", NP, TW)]:
        s = send(name, kind, a, b, s)
    for t in range(4):
        vec("l0%d" % t, lambda e, q, t=t: q.tensor_scalar(B("l0", 24 * t, 24 * t + 24), T.sti[:], 4.0, float(t), MUL, ADD),
            [("sti", 0, 24)], [("l0", 24 * t, 24 * t + 24)])

    def hop(t, c):
        a, b = CH[c]
        n, la, lb, k0 = b - a, a // 16, b // 16, 4 * c
        m, tag = lb - la, "%d%d" % (t, c)
        z, zn, bl, bt, rt = "z%d" % t, "z%d" % (t + 1), "bl%d" % t, "bt%d" % t, "rt%d" % t

        def bank(i):
            return B("ps", 512 * (k0 + i), 512 * (k0 + i) + n)
        if t == 0:
            for i in range(4):
                op("kg%d%d" % (c, i), "VS", ("g", n),
                   moved(lambda i=i: B("kg", 4 * a + i, 4 * b, 4), lambda i=i: T.kt[:].indirect(B("l0", 24 * i + la, 24 * i + lb))),
                   [("kt", 0, 4 * NP), ("l0", 24 * i + la, 24 * i + lb)], [("kg", 4 * a, 4 * b, i)])
            quant("qg%d" % c, "ng", a, b, "kg", 4 * a)
            quant("qx%d" % c, "z0", a, b, "xt", 4 * a)
            terms = [("ea", "ng", a), ("ea", "z0", a)]
        else:
            for h, x0 in enumerate((2 * a, a + b)):
                pick("pe%s%d" % (tag, h), "pk%d" % t, x0, x0 + n, "tb%d" % t, 0, NP, "lp%d" % t, x0 // 16, ["a%dt" % t])
            terms = [("ea", z, a), ("ee", "pk%d" % t, 2 * a), ("eo", "pk%d" % t, a + b)]
        for j, (st, mv, m0) in enumerate(terms):
            for i in range(4):
                mm("mb%s%d%d" % (tag, j, i), k0 + i, st, 128 * i, mv, m0, m0 + n, j == 0, j == len(terms) - 1, grp="b%s%d" % (tag, i))
        for i in range(4):
            op("eb%s%d" % (tag, i), "VS", ("e", n), affine(lambda i=i: B(bt, 4 * a + i, 4 * b, 4), lambda i=i: bank(i), 0.5),
               [], [("ps", k0 + i, k0 + i + 1), (bt, 4 * a, 4 * b, i)])
        quant("qb" + tag, bl, a, b, bt, 4 * a)
        mm("ms" + tag, k0, "tb%d" % t, NP, bl, a, b, True, True, arr=["a%duq" % t, "a%dus" % t] if t else [])
        bit, sa, lf, ln, pn = ["%s%d" % (s, t) for s in ("bit", "sa", "lf", "ln", "pn")]
        op("gt" + tag, "S", ("e", n), lambda e, q: q.activation(B(bit, a, b), bank(0), ActivationFunctionType.Sign, bias=-2.0 ** -120),
           [], [("ps", k0, k0 + 1), (bit, a, b)])
        vec("sa" + tag, lambda e, q: q.tensor_tensor_scan(B(sa, a, b), B(bit, a, b), B("wt", 0, n), 0.0, ADD, MUL),
            [("wt", 0, 1), (bit, a, b)], [(sa, a, b)], n // 2)
        rep = 2 if t < NH - 1 else 1
        f0, f1 = 2 * la, 2 * la + rep * m
        for r in range(rep):
            vec("lf%s%d" % (tag, r), lambda e, q, r=r: q.tensor_tensor(B(lf, f0 + r, f1, rep), B(sa, a + 15, b, 16), B(pn, 2 * la + 1, 2 * lb, 2), ADD),
                [(sa, a, b), (pn, 2 * la, 2 * lb)], [(lf, f0, f1, r)])
        vec("ln" + tag, lambda e, q: q.tensor_scalar(B(ln, f0, f1), B(lf, f0, f1), 8.0, T.cl[:], MUL, ADD),
            [(lf, f0, f1), ("cl", 0, 1)], [(ln, f0, f1)])
        if t == NH - 1:
            op("pl" + tag, "VS", ("g", n), affine(lambda: B("plb", a, b), lambda: T.wb[:].indirect(B(ln, f0, f1)), 4.0, MID),
               [("wb", 0, 2 * NP), (ln, f0, f1)], [("plb", a, b)])
        else:
            gm, sb, lp, nb = ["%s%d" % (s, t + 1) for s in ("gm", "sb", "lp", "pn")]
            op("gm" + tag, "VS", ("g", 2 * n), moved(lambda: B(gm, 2 * a, 2 * b), lambda: T.wb[:].indirect(B(ln, f0, f1))),
               [("wb", 0, 2 * NP), (ln, f0, f1)], [(gm, 2 * a, 2 * b)])
            vec("sb" + tag, lambda e, q: q.transpose(B(sb, 2 * a, 2 * b), B(gm, 2 * a, 2 * b)), [(gm, 2 * a, 2 * b)], [(sb, 2 * a, 2 * b)], n)
            for h in range(2):
                x0 = 2 * la + h * m
                vec("lp%s%d" % (tag, h),
                    lambda e, q, x0=x0, h=h: q.tensor_scalar(B(lp, x0, x0 + m), B(sb, 2 * a + 16 * h + t, 2 * b, 32), 4.0, MID, MUL, ADD),
                    [(sb, 2 * a, 2 * b)], [(lp, x0, x0 + m)])
            vec("ph" + tag, lambda e, q: q.tensor_tensor_scan(B(nb, 2 * la, 2 * lb), B("dd", 0, 2 * m), B(sb, 2 * a + t, 2 * b, 16), 0.0,
                                                              ADD, AluOpType.max),
                [(sb, 2 * a, 2 * b), ("dd", 0, 1)], [(nb, 2 * la, 2 * lb)])
        for i in (1, 2, 3, 0):
            mm("mr%s%d" % (tag, i), k0 + i, "ww", 128 * i, bl, a, b, True, True)
            op("er%s%d" % (tag, i), "VS", ("e", n), affine(lambda i=i: B(rt, 4 * a + i, 4 * b, 4), lambda i=i: bank(i), 0.03125),
               [], [("ps", k0 + i, k0 + i + 1), (rt, 4 * a, 4 * b, i)])
        quant("qz" + tag, zn, a, b, rt, 4 * a)
        if t == NH - 1:
            mm("my%d" % c, k0 + 1, "vv", 0, zn, a, b, True, True)
            op("ey%d" % c, "VS", ("e", n), moved(lambda: B("yb", a, b), lambda: bank(1)), [], [("ps", k0 + 1, k0 + 2), ("yb", a, b)])
            dma("sty%d" % c, "YS", lambda: (B("y", a, b), B("yb", a, b)), 512 * n, 128, [("yb", a, b)], [])
            dma("stc%d" % c, "YS", lambda: (B("oc", 4 * a, 4 * b), u8(zn + "q", a, b)), 512 * n, 128, [(zn + "q", a, b)], [])

    for t in range(NH):
        for c in range(2):
            hop(t, c)
        if t < NH - 1:
            l = rows(t + 1, l, ["a%dn" % (t + 1)])
        if t == 0:
            l = [dma("ldv", "Y", lambda: (T.vt[:], T.v[:]), 131072, 128, [], [("vt", 0, 512)], l)]
            quant("qv", "vv", 0, 128, "vt", 0)
    for k in range(4):
        dma("sts%d" % k, "YS", lambda k=k: (T.osc[4 * k:4 * k + 4, :], T.z3s[32 * k:32 * k + 4, :]), 1536, 4, [("z3s", 0, NT)], [])
    dma("stp", "YS", lambda: (T.pl[:], T.plb[NH - 1:128:16, :]), 12288, 16, [("plb", 0, NT)], [])
    return ops


PIECES = ["n", "tq", "ts", "uq", "us"]
ARR = {w + p: ("h" if w == "a2" else "s") + p for w in ("a1", "a2", "ah") for p in PIECES}


def overlap(r, s):
    if r[0] != s[0] or r[2] <= s[1] or s[2] <= r[1]:
        return False
    return len(r) < 4 or len(s) < 4 or r[3] == s[3]


def link(ops):
    for i, o in enumerate(ops):
        o["dep"] = [j for j, p in enumerate(ops[:i]) if (o["grp"] is None or o["grp"] != p["grp"]) and (
            any(overlap(r, s) for r in o["R"] + o["W"] for s in p["W"]) or any(overlap(r, s) for r in o["W"] for s in p["R"]))]
    return ops


ORDER = """
0S 9G 8G 11V 15V 16V 17V 18V 12V 20V 19V 10G 35V 13V 23V 34V 26S 24S 36S 14S 41S 27S 1Y 2Y 3Y 4Y 5Y 6Y 7Y 62V 32V 21V 64V 48Y 28V 61V 37V 63V 33V 107V 104V 105S 106S 65S 66S 68S 67S 49V 108V 70V 109V 44V 42V 69V 25S 111P 113P 110P 112P 116P 117P 114P 115P 120S 121S 119S 118S 74P 73P 71P 78P 77P 72P 76P 75P 50V 22V 51V 29V 122V 31V 30V 39V 80V 40V 52S 82S 81S 79S 83V 123P 138P 134P 136P 124S 140P 135S 137S 141S 84P 85S 95P 97P 101P 99P 46G 53G 55G 57G 59G 47H 54H 56H 58H 60H 125V 139V 127V 126V 45V 128V 38V 86V 142V 88V 87V 96S 192P 191P 193P 194P 98S 129S 102S 100V 89V 130V 90S 103V 131V 132V 187V 152P 151P 150P 153P 188S 190S 91V 189V 92V 93V 43V 146V 147S 196P 197P 198P 195P 202P 201P 199P 200P 149S 206S 204S 148V 154P 155P 156P 159P 157P 161P 160P 158P 163S 165S 164S 203V 205V 133V 207V 94V 162V 166V 143Y 208P 223P 221P 219P 209S 225P 224S 220S 226S 167P 168S 178P 182P 180P 184P 210V 222V 212V 211V 213V 179S 214S 181S 227V 169V 183V 171V 170V 185V 172V 173S 144Y 228Y 215V 186V 216V 217V 269V 273P 274P 276P 275P 270S 272S 174V 271V 234P 236P 235P 233P 175V 230S 177V 176V 229V 280P 277P 278P 279P 283P 282P 281P 284P 232S 286S 288S 231V 239P 240P 238P 243P 244P 237P 241P 242P 247S 287V 285V 218V 289V 145V 290P 248S 245S 246V 249V 291S 300P 296P 298P 301V 302P 297S 299S 303V 292V 304V 250P 258P 260P 256P 251S 261S 259S 262P 257V 263V 252V 264V 253V 293V 254V 294V 305P 265P 308Y 306S 307S 266V 309Y 255V 311S 312S 268Y 310Y 267Y 295S 313S
"""
_OPS = build(None, None, None)
PLAN = [(int(w[:-1]), w[-1]) for w in ORDER.split()]
SEMAPHORES = ["cV", "cS", "cP", "cG", "sent"] + sorted(ARR) + ["d" + o["name"] for o in _OPS if o["kind"] == "dma"]


def rank_program(g, core, T, topo):
    n = len(T.cores)
    rank = T.rank_of(core)
    served = [r for r in range(n) if helper(T, topo, r) == core]
    if rank is None and not served:
        return
    if served:
        rank = served[0]
        src, to = T.cores[rank], T.cores[(rank - 2) % n]
        came = len(topo.engines(src, core)) - len(topo.engines(src, T.cores[(rank - 1) % n]))
        ops = build(T, topo, rank)
        steps = [ops[i] for i, e in PLAN if e == "H"]
        for o in steps:
            g.wait_ge(T.sem[o["arr"][0]], came)
            o["fn"]("H", g)
        g.wait_ge(T.sem.sent, len(steps) * len(topo.engines(core, to)))
        return
    ops = link(build(T, topo, rank))
    far = {"a1": T.cores[(rank + 1) % n], "a2": helper(T, topo, (rank + 2) % n)}
    arrive = {a: len(topo.engines(far[a[:2]], core)) for a in ARR if a[:2] in far}
    queue = {"V": g.vector, "S": g.scalar, "P": g.tensor, "G": g, "Y": g.sync}
    known = {e: {} for e in queue}
    count, event = dict(arrive), {}
    for i, e in PLAN:
        if e == "H":
            continue
        o, q, kn = ops[i], queue[e], known[e]
        top = {}
        for s, v, clock in [event[j] for j in o["dep"]] + [(a, arrive[a], {}) for a in o["arr"]]:
            if v > top.get(s, (0, None))[0]:
                top[s] = (v, clock)
        for s in sorted(top, key=lambda s: -len(top[s][1])):
            v, clock = top[s]
            if kn.get(s, 0) < v:
                q.wait_ge(T.sem[s], v)
                kn[s] = v
                for s2, v2 in clock.items():
                    kn[s2] = max(kn.get(s2, 0), v2)
        ins = o["fn"](e, q)
        if o["kind"] == "rem":
            s, inc = "sent", len(topo.engines(core, helper(T, topo, rank)))
        else:
            s, inc = ("c" + e, 1) if o["kind"] == "c" else ("d" + o["name"], 16)
            ins.then_inc(T.sem[s], inc)
        count[s] = count.get(s, 0) + inc
        event[i] = (s, count[s], dict(kn))
    last = {s: k for k, (s, v, clock) in enumerate([event[i] for i, e in PLAN if e != "H"])}
    for s in sorted(count, key=lambda s: last.get(s, -1)):
        g.wait_ge(T.sem[s], count[s])
